import numpy as np, ml_dtypes
CORES = [36,164,52,180,100,228,116,244]
N = 8
import mx_ref
BF = ml_dtypes.bfloat16
def entries(a):
    return np.ascontiguousarray(a.T).reshape(-1)
def table(e):
    return np.ascontiguousarray(np.reshape(e, (-1, 16)).T).astype(np.int32)
def gentries(a):
    return np.ascontiguousarray(a.reshape(8, 16, -1).transpose(0, 2, 1)).reshape(8, -1)
def gtable(e):
    e = np.asarray(e); return np.ascontiguousarray(e.reshape(8, -1, 16).transpose(0, 2, 1)).reshape(128, -1).astype(np.int32)
def gcols(t, e):
    v = np.concatenate([t.reshape(8, 16, -1, 4), np.zeros((8, 16, 1, 4), BF)], axis=2)
    return np.ascontiguousarray(np.stack([v[g][:, e[g]] for g in range(8)])).reshape(128, -1)
def tile(rs):
    return np.stack(rs, axis=2).reshape(128, -1).astype(BF)
def pick(q, e):
    c = np.concatenate([q[0].reshape(128, -1, 4), np.zeros((128, 1, 4), np.uint8)], axis=1); s = np.concatenate([q[1], np.ones((16, 1), np.uint8)], axis=1)
    return (np.ascontiguousarray(c[:, e].reshape(128, -1)), np.ascontiguousarray(s[:, e]))
def join(*qs):
    return (np.concatenate([q[0] for q in qs], axis=1), np.concatenate([q[1] for q in qs], axis=1))
def put(q, e, v):
    c, s = q[0].reshape(128, -1, 4).copy(), q[1].copy(); c[:, e] = v[0].reshape(128, -1, 4); s[:, e] = v[1]
    return (c.reshape(128, -1), s)
def pk(c, s):
    return (np.ascontiguousarray(c), mx_ref.live(s))
def emit(q):
    return q[0], q[1]
def packed(v, rng):
    q = [mx_ref.quantize(np.ascontiguousarray(v[r])) for r in range(N)]
    return np.stack([a for a, b in q]), np.stack([mx_ref.plane(b, rng) for a, b in q])
def values_of_codes():
    e, c = np.zeros((128, 128, 4), np.float32), np.zeros((128, 2, 4), np.uint8)
    e[np.arange(128), np.arange(128), 0] = 1
    c[:127, :, 0] = np.arange(256).reshape(2, 128).T[:127]
    return mx_ref.matmul(mx_ref.quantize(e.reshape(128, 512).astype(BF)), (c.reshape(128, 8), np.full((16, 2), 127, np.uint8))).T.reshape(-1).astype(np.float64)
CODE_VALUE, SCALE_VALUE = values_of_codes(), 2.0 ** (np.arange(256) - 127.0)
def decode(q):
    return (CODE_VALUE[q[0]].reshape(16, 8, -1, 4) * SCALE_VALUE[q[1]][:, None, :, None] + 0.0).reshape(128, -1).astype(np.float32)
def f(rng, *shape):
    return mx_ref.flush((rng.standard_normal(shape, dtype=np.float32) * np.exp2(rng.integers(-2, 3, shape[:-1] + (1,)))).astype(BF))
def wide(rng, *shape, cols=0):
    v = rng.standard_normal(shape, dtype=np.float32) * np.exp2(rng.integers(-12, 13, shape)).astype(np.float32)
    if cols: v *= np.repeat(np.exp2(rng.integers(-cols, cols + 1, shape[:-2] + (1, shape[-1] // 4))) * (rng.random(shape[:-2] + (1, shape[-1] // 4)) > 0.0625), 4, axis=-1).astype(np.float32)
    return mx_ref.flush(v.astype(BF))
C, K, M = 448, 64, 7
DIST = [1, 2, 4]
def big(v):
    v = v.astype(np.float32)
    v[np.abs(v) < np.float32(2.0 ** -16)] = 0
    return v.astype(BF)
def numbers_of(rng):
    return {"x": big(f(rng, N, 128, 4 * C)), "u": np.array(f(rng, N, 128, 512)), "v": np.array(f(rng, N, 128, 512))}
def trees(rng):
    j = np.arange(C)
    return np.maximum(j - 1 - np.floor(rng.random((N, C)) ** 3 * j).astype(np.int64), 0)
def flags(rng):
    a = (rng.random((N, 8, C)) < 0.5) * 1
    a[:, :, 0] = 1
    return a
def lists_of(e, a):
    return {"par": np.stack([table(e[r]) for r in range(N)]), "fl": np.stack([gtable(a[r]) for r in range(N)])}
def layers(rng):
    return big(f(rng, N, 128, 2048)).reshape(N, 8, 16, 4, 8, 16, 4)
def carry(w, parts, k):
    k = np.asarray(k, np.float32).astype(BF)
    w[:, :, :, :, :, parts] = 0
    for g in range(8):
        for i in parts:
            for b in range(4): w[:, g, i, b, g, i, b] = k[:, g]
    return w
def weights(rng, w):
    c, p = packed(np.ascontiguousarray(w).reshape(N, 128, 2048), rng)
    return {"wc": c, "ws": p}
def setup_inputs(rng):
    return {**numbers_of(rng), **lists_of(trees(rng), flags(rng)), **weights(rng, layers(rng))}
def setup_inputs_ties(rng):
    d = numbers_of(rng)
    first = int(rng.integers(N))
    ones = [(first + 1) % N, (first + 2) % N]
    x = d["x"].reshape(N, 8, 16, C, 4)
    for r in range(N):
        a = x[r][:, :8, :3].copy()
        a[:, :, 2] = 0
        x[r][:, :8] = a[:, :, rng.permutation(C) % 3]
    x[first, :, :8] = 0
    x[ones, :, :8] = 1
    u = d["u"].reshape(N, 8, 16, 128, 4)
    z = u.copy()
    u[:, :, :, ::16] = 0
    u[:, :, :, 1::16] = 0
    for g in range(8):
        for i in (16 * g, 16 * g + 1):
            u[:, g, :8, i] = z[:, g, :8, i]
            for r in ones: u[r, g, :8, i] = np.abs(z[r, g, :8, i])
    w = carry(layers(rng), list(range(8)), np.full((N, 8), 32.0))
    return {"x": x.reshape(N, 128, 4 * C), "u": u.reshape(N, 128, 512), "v": d["v"], **lists_of(trees(rng), flags(rng)), **weights(rng, w)}
def setup_inputs_near(rng):
    d = numbers_of(rng)
    x = np.zeros((N, 8, 16, C, 4), np.float32)
    a = (N, 8, 8, C, 4)
    x[:, :, 8:] = rng.choice([-1.0, 1.0], a) * (1.0 + (2 * rng.integers(0, 64, a) + 1) * 2.0 ** -7) * np.exp2(-rng.integers(8, 15, a).astype(np.float64))
    x[:, :, 8 + int(rng.integers(8)), :, int(rng.integers(4))] = np.where(np.arange(8) % 2 == 1, 1.75, 1.96875)[None, :, None]
    x[:, :, 8:] *= np.exp2(rng.integers(-1, 2, (N, 8, 1, C, 1)).astype(np.float32))
    u = d["u"].reshape(N, 128, 128, 4)
    u[:, :, ::16] = 0
    u[:, :, 1::16] = 0
    o = rng.permutation(N) % 2
    m = flags(rng)
    for r in range(N):
        k = 2.0 ** -30 if o[r] == 0 else 1.0
        s = rng.integers(-1, 2, (8, 2, C)) * k
        t = np.concatenate([1.125 * s, -1.25 * s], axis=1)
        for g in rng.permutation(8)[:4]:
            j = int(rng.integers(C))
            t[g, :2, j] = 2.0 ** 30 * rng.choice([-1.0, 1.0], 2)
            t[g, 2:, j] = 0
            m[r, g, j] = 1
        x[r, :, :4, :, 0] = t
        for h in range(0, 128, 16):
            for b in range(2):
                u[r, h + b, h + b, 0] = 1.125 * k
                u[r, h + 2 + b, h + b, 0] = k
    w = np.zeros((N, 8, 16, 4, 8, 16, 4), np.float32).astype(BF)
    w = carry(w, list(range(8)), np.full((N, 8), 32.0))
    w = carry(w, list(range(8, 16)), np.where(np.arange(8) % 2 == 1, 36.0, 32.0) * np.ones((N, 1)))
    return {"x": x.reshape(N, 128, 4 * C).astype(BF), "u": u.reshape(N, 128, 512), "v": d["v"], **lists_of(trees(rng), m), **weights(rng, w)}
def setup_inputs_chain(rng):
    d = numbers_of(rng)
    u = d["u"].reshape(N, 128, 128, 4)
    g = int(rng.integers(8))
    u[:, :, 16 * g:16 * g + 2] = 0
    d["u"] = u.reshape(N, 128, 512)
    o = rng.permutation(N) % 4
    e = np.stack([np.maximum(np.arange(C) - 1, 0)] * N)
    m = np.zeros((N, 8, C), np.int64)
    for r in range(N):
        if o[r] == 1: m[r, np.arange(8), rng.integers(1, C // 4, 8)] = 1
        if o[r] == 2:
            e[r] = 0
            m[r, rng.permutation(8)[:4]] = 1
        if o[r] == 3: m[r] = 1
    m[:, :, 0] = 1
    return {**d, **lists_of(e, m), **weights(rng, layers(rng))}
def setup_inputs_huge(rng):
    d = numbers_of(rng)
    c = rng.choice([-1.0, 1.0], (N, 8, 1, C, 1))
    c[int(rng.integers(N))] = -1
    x = c * (0.8 + 0.2 * rng.random((N, 8, 16, C, 4))) * 2.0 ** 30
    u = d["u"].reshape(N, 8, 16, 128, 4)
    u[:, :, :, ::16] = 0
    u[:, :, :, 1::16] = 0
    for g in range(8):
        for b in range(2):
            for h in rng.permutation(8)[:1 + 2 * ((g + b) % 4)]:
                u[:, h, :, 16 * g + b] = (2.0 ** 30 * (0.9 + 0.1 * rng.random((N, 16, 4)))).astype(np.float32).astype(BF)
    w = carry(np.zeros((N, 8, 16, 4, 8, 16, 4), np.float32).astype(BF), list(range(16)), 32.0 * rng.choice([-1.0, 1.0], (N, 8)))
    return {"x": x.astype(np.float32).reshape(N, 128, 4 * C).astype(BF), "u": u.reshape(N, 128, 512), "v": d["v"], **lists_of(trees(rng), flags(rng)), **weights(rng, w)}
def setup_inputs_spread(rng):
    d = setup_inputs(rng)
    d["x"] = big(wide(rng, N, 128, 4 * C, cols=6))
    return d
def check_inputs(d):
    b = []
    for k in ("x", "u", "v"):
        a = np.abs(d[k].astype(np.float32))
        if not (np.isfinite(a).all() and ((a == 0) | (a >= 2.0 ** -30) & (a <= 2.0 ** 30)).all()): b.append("a value of " + k)
    none, least, most = [emit(mx_ref.quantize(np.full((128, 16), k, np.float32).astype(BF)))[1][0, 0] for k in (0.0, 2.0 ** -30, 2.0 ** 30)]
    for r in range(N):
        e = entries(d["par"][r])
        if e[0] != 0 or ((e[1:] < 0) | (e[1:] >= np.arange(1, C))).any(): b.append("par: an entry out of range")
        m = gentries(d["fl"][r])
        if ((m != 0) & (m != 1)).any(): b.append("fl: an entry that is neither 0 nor 1")
        if (m[:, 0] != 1).any(): b.append("fl: column 0 isn't flagged in every group")
        if ((d["wc"][r] == 0x7F) | (d["wc"][r] == 0xFF)).any(): b.append("wc: a code that is no number")
        s = mx_ref.live(d["ws"][r])
        if ((s != none) & ((s < least) | (s > most))).any(): b.append("ws: a scale out of range")
    return b
def inherited(now, flag, up):
    a = np.where(flag == 1, np.arange(C), up[:, None])
    for i in range(9): a = np.take_along_axis(a, a, axis=2)
    return [gcols(now[r], a[r]) for r in range(N)]
def reference(x, u, v, par, fl, wc, ws):
    qu = [mx_ref.quantize(u[r]) for r in range(N)]
    lay = [pk(wc[r], ws[r]) for r in range(N)]
    now = [x[r] for r in range(N)]
    up = np.stack([entries(par[r]) for r in range(N)])
    flag = np.stack([gentries(fl[r]) for r in range(N)])
    for h in DIST:
        e = inherited(now, flag, up)
        sym, came, new = [], [], []
        for r in range(N):
            q = mx_ref.quantize(e[r])
            s = mx_ref.matmul(qu[r], q)
            sym.append(2 * (s[::16] > 0) + (s[1::16] > 0))
            k = pick(q, np.arange(0, C, M))
            t = tile([mx_ref.matmul(pick(lay[r], np.arange(128 * b, 128 * b + 128)), k) * np.float32(0.03125) for b in range(4)])
            came.append(decode(mx_ref.quantize(t)).astype(BF))
        for r in range(N):
            d = (r + h) % N
            key, lock = sym[d][:, ::M], sym[r]
            master = lock[:, up[r]]
            agree = (key[:, None] == lock[:, :, None]) | (key[:, None] == master[:, :, None])
            best = np.argmax(np.count_nonzero(agree, axis=0), axis=1)
            far = key[:, best]
            wanted = (far != lock) & (far != master)
            left = (far != lock) & (far == master)
            new.append(gcols(np.concatenate([now[r], came[d]], axis=1), np.where(wanted, C + best, np.arange(C))))
            flag[r] = np.where(wanted, 1, np.where(left, 0, flag[r]))
        now = new
    e = inherited(now, flag, up)
    y, ofl = np.zeros((N, 128, C), np.float32), np.zeros((N, 8, C), np.float32)
    oc, osc = np.zeros((N, 128, 4 * C), np.uint8), np.zeros((N, 16, C), np.uint8)
    for r in range(N):
        q = mx_ref.quantize(e[r])
        y[r] = mx_ref.matmul(mx_ref.quantize(v[r]), q)
        ofl[r] = flag[r]
        oc[r], osc[r] = emit(q)
    return {"y": y, "ofl": ofl, "oc": oc, "osc": osc}

@@ -1,0 +1,653 @@
+from concourse.mybir import dt, AluOpType, ActivationFunctionType
+
+F32, BF, I32, U16, X4, U8 = "float32", "bfloat16", "int32", "uint16", "float8_e4m3fn_x4", "uint8"
+_S = {
+    "xl": (1792, BF), "pl": (2560, BF), "ul": (512, BF), "vl": (512, BF), "zz": (1024, BF),
+    "qu": (128, X4), "su": (128, U8), "qua": (128, X4), "sua": (128, U8), "qub": (128, X4), "sub": (128, U8),
+    "qv": (128, X4), "sv": (128, U8), "qw": (512, X4), "sw": (512, U8),
+    "et": (2304, BF), "qe": (576, X4), "se": (576, U8), "bt": (768, BF), "qb": (192, X4), "sb": (192, U8),
+    "ht": (512, BF), "qh0": (128, X4), "sh0": (128, U8), "qh1": (128, X4), "sh1": (128, U8), "qh2": (128, X4), "sh2": (128, U8),
+    "lq": (320, X4), "ls": (320, U8), "ab": (896, BF), "oh": (896, BF), "d01": (512, BF),
+    "at": (1920, BF), "qa": (480, X4), "sa": (480, U8), "ct": (704, BF), "qc": (176, X4), "sc": (176, U8),
+    "dc": (2048, BF), "qd": (512, X4), "sd": (512, U8), "one": (512, BF), "q1": (128, X4), "s1": (128, U8),
+    "tb": (704, F32), "so0": (16, U16), "so1": (16, U16), "so2": (16, U16), "lo0": (16, U16), "lo1": (16, U16), "lo2": (16, U16),
+    "kc": (192, F32), "g0": (256, F32), "g1": (256, F32), "tt": (320, F32), "hh": (240, F32), "dd": (240, F32), "ro": (780, F32),
+    "ri": (16, I32), "fi": (48, I32), "ni": (16, I32), "sm": (48 * 12, F32),
+    "pre": (64, F32), "c1p": (64, F32), "va": (64, F32), "vb": (64, F32), "v0": (64, F32), "vz": (144, F32), "tk": (80, F32),
+    "wa": (144, F32), "wb": (272, F32), "wx": (448, F32), "l1": (128, F32), "fin": (160, F32), "tw": (288, F32),
+    "pk": (32, F32), "pkf": (32, F32), "hub": (32, F32), "ks": (32, F32),
+    "oe": (36, U16), "pw": (32, I32), "pall": (32, F32), "pq": (96, F32), "pa": (64, F32), "pb": (64, F32), "xa": (64, F32),
+    "xb": (64, F32), "xz": (128, F32), "xy": (128, F32), "xw": (128, F32), "tx": (80, F32),
+    "sx": (256, F32), "op": (80, U16), "om": (32, U16), "pi": (160, I32), "pf": (96, F32),
+    "fw": (32, I32), "ff": (32, F32), "fc": (32, F32), "fe": (128, F32), "ft": (128, F32), "f2": (128, F32), "fo": (64, F32), "yo": (448, F32),
+    "iot": (448, F32), "ci": (16, I32), "cf": (16, F32), "cd": (64, F32), "j16": (192, F32), "zj": (128, I32),
+    "ma": (192, F32), "mb": (32, F32), "mc": (256, F32), "m16": (128, F32), "mk": (192, F32), "m7": (32, F32), "jq": (192, F32), "hk": (64, F32),
+    "jb": (64 * 3, F32), "io": (192, F32), "z7": (64, I32), "z8": (64, I32), "lu": (80, U16), "c3": (48, F32), "c3i": (8, I32),
+}
+SCRATCH = {k: ("sbuf", [128, n], d) for k, (n, d) in _S.items()}
+SCRATCH["ps"] = ("psum", [128, 4096], F32)
+SEMAPHORES = ["cv", "cs", "cp", "cg", "sent"] + ["d%d" % k for k in range(44)] + ["ar0", "ar1", "ar2", "ah0", "ah1", "ah2"]
+
+DIST = [1, 2, 4]
+A = AluOpType
+AF = ActivationFunctionType
+BIG = -4000000.0
+TINY = 2.0 ** -120
+
+
+def rank_program(g, core, T, topo):
+    rank = T.rank_of(core)
+    if rank is None:
+        return
+    n_ranks = len(T.cores)
+    Q = {"v": g.vector, "s": g.scalar, "p": g.tensor, "g": g, "y": g.sync}
+    SEM = {"v": "cv", "s": "cs", "p": "cp", "g": "cg"}
+    count = {"cv": 0, "cs": 0, "cp": 0, "cg": 0, "sent": 0}
+    waited = {k: {} for k in Q}
+    hist = {}
+    nd = [0]
+
+    def R(name, c0=0, c1=None, step=1, p0=0, p1=128):
+        if c1 is None:
+            c1 = 4096 if name == "ps" else _S[name][0]
+        ap = T[name][p0:p1, c0:c1:step] if step > 1 else T[name][p0:p1, c0:c1]
+        if name == "ps":
+            return (ap, [("ps", 0, 128, c0 // 512 * 512, c0 // 512 * 512 + 512, 1)])
+        return (ap, [(name, p0, p1, c0, c1, step)])
+
+    def IND(w, o):
+        return (w[0].indirect(o[0]), w[1] + o[1])
+
+    def CAST(v, d):
+        return (v[0].bitcast(d), v[1])
+
+    def meet(a, b):
+        if a[1] >= b[2] or b[1] >= a[2] or a[3] >= b[4] or b[3] >= a[4]:
+            return False
+        return not (a[5] == b[5] and a[5] > 1 and (a[3] - b[3]) % a[5])
+
+    def wait(e, tok):
+        if waited[e].get(tok[0], 0) < tok[1]:
+            Q[e].wait_ge(T.sem[tok[0]], tok[1])
+            waited[e][tok[0]] = tok[1]
+
+    def deps(e, reads, writes):
+        need = {}
+        for regs, wr in ((reads, False), (writes, True)):
+            for r in regs:
+                for (h, tok, hw) in hist.get(r[0], []):
+                    if (wr or hw or (r[0] == "ps" and tok[0] != SEM.get(e))) and meet(r, h):
+                        need[tok[0]] = max(need.get(tok[0], 0), tok[1])
+        for s, v in need.items():
+            wait(e, (s, v))
+
+    def note(reads, writes, tok):
+        for r in reads:
+            hist.setdefault(r[0], []).append((r, tok, False))
+        for r in writes:
+            hist.setdefault(r[0], []).append((r, tok, True))
+
+    def run(e, fn, ins, outs):
+        reads = [r for v in ins if isinstance(v, tuple) for r in v[1]]
+        writes = [r for v in outs for r in v[1]]
+        deps(e, reads, writes)
+        s = SEM[e]
+        count[s] += 1
+        fn().then_inc(T.sem[s], 1)
+        note(reads, writes, (s, count[s]))
+
+    def ap(v):
+        return v[0] if isinstance(v, tuple) else v
+
+    def dma(e, out, in_):
+        reads = in_[1] if isinstance(in_, tuple) else []
+        writes = out[1] if isinstance(out, tuple) else []
+        deps(e, reads, writes)
+        s = "d%d" % nd[0]
+        nd[0] += 1
+        count[s] = 16
+        Q[e].dma_start(ap(out), ap(in_)).then_inc(T.sem[s], 16)
+        note(reads, writes, (s, 16))
+
+    def cp(o, i):
+        run("v", lambda: g.vector.tensor_copy(o[0], i[0]), [i], [o])
+
+    def tt(o, a, b, op):
+        run("v", lambda: g.vector.tensor_tensor(o[0], a[0], b[0], op), [a, b], [o])
+
+    def ts(o, a, s1, op0, s2=None, op1=None):
+        if op1 is None:
+            run("v", lambda: g.vector.tensor_scalar(o[0], a[0], ap(s1), None, op0), [a, s1], [o])
+        else:
+            run("v", lambda: g.vector.tensor_scalar(o[0], a[0], ap(s1), ap(s2), op0, op1), [a, s1, s2], [o])
+
+    def scan(o, d0, d1, init, op0, op1):
+        run("v", lambda: g.vector.tensor_tensor_scan(o[0], d0[0], d1[0], init, op0, op1), [d0, d1], [o])
+
+    def tr(o, i):
+        run("v", lambda: g.vector.transpose(o[0], i[0]), [i], [o])
+
+    def ms(o, c):
+        run("v", lambda: g.vector.memset(o[0], c), [], [o])
+
+    def qz(q, s, i):
+        run("v", lambda: g.vector.quantize_mx(q[0], s[0], i[0]), [i], [q, s])
+
+    def act(o, i, f=AF.Copy, scale=None, bias=None):
+        kw = {}
+        if scale is not None:
+            kw["scale"] = ap(scale)
+        if bias is not None:
+            kw["bias"] = ap(bias)
+        run("s", lambda: g.scalar.activation(o[0], i[0], f, **kw), [i, scale, bias], [o])
+
+    def lin(o, i, scale, bias):
+        act(o, i, AF.Identity, scale, bias)
+
+    def mm(bank, n, lq, ls, rq, rs):
+        o = R("ps", 512 * bank, 512 * bank + n)
+        run("p", lambda: g.tensor.matmul_mx(o[0], lq[0], ls[0], rq[0], rs[0], True, True), [lq, ls, rq, rs], [o])
+
+    def iota(o, pat, base, cm, small=True):
+        if small:
+            run("g", lambda: g.iota(o[0], pat, base, cm, allow_small_or_imprecise_dtypes=True), [], [o])
+        else:
+            run("g", lambda: g.iota(o[0], pat, base, cm), [], [o])
+
+    def send(o, i, sem, dst):
+        deps("g", i[1], [])
+        rid, pid = topo.addr(dst, core)
+        g.remote_dma(o, i[0], T.sem[sem], T.sem["sent"], pid, rid, topo.mask(core, dst))
+        count["sent"] += len(topo.engines(core, dst))
+
+    def PS(bank, c0, c1):
+        return R("ps", 512 * bank + c0, 512 * bank + c1)
+
+    def col(name, c):
+        return R(name, c, c + 1)
+
+    def quad(name, q, c0, c1, step=1):
+        return R(name, c0, c1, step, 32 * q, 32 * q + 32)
+
+    def either(k, o, i):
+        if k % 2:
+            act(o, i)
+        else:
+            cp(o, i)
+
+    dma("y", R("pw", 0, 28, 1, 0, 16), T.par[:])
+    dma("s", R("pw", 0, 28, 1, 16, 32), T.par[:])
+    dma("y", R("fw", 0, 28), T.fl[:])
+    dma("s", R("xl", 0, 896), T.x[:, 0:896])
+    dma("y", R("xl", 896, 1792), T.x[:, 896:1792])
+    dma("y", R("ul"), T.u[:])
+    dma("y", CAST(R("qw"), dt.uint8), T.wc[:])
+    dma("y", R("sw"), T.ws[:])
+    dma("y", R("vl"), T.v[:])
+
+    iota(col("ci", 0), [[0, 1]], 0, 1, False)
+    iota(col("ci", 1), [[0, 1]], 0, 7, False)
+    iota(R("j16"), [[0, 12], [1, 16]], 0, 0)
+    iota(R("iot"), [[1, 448]], 0, 0)
+    iota(R("io", 0, 8), [[2, 2], [1, 2], [4, 2]], 0, 0)
+    iota(R("io", 16, 20), [[9, 2], [18, 2]], 0, 0)
+    iota(R("io", 32, 60), [[0, 4], [1, 7]], 0, 0)
+    iota(R("vz", 0, 16), [[0, 16]], 0, 0)
+    iota(R("tk", 64, 80), [[0, 16]], 0, 0)
+    iota(R("tx", 64, 80), [[0, 16]], 0, 0)
+    iota(R("zz"), [[0, 1024]], 0, 0)
+    iota(R("wa"), [[0, 144]], 0, 0)
+    iota(R("wb"), [[0, 272]], 0, 0)
+    iota(R("fin"), [[0, 160]], 0, 0)
+    iota(R("io", 64, 118), [[32, 6], [0, 9]], 0, 0)
+    iota(R("z7"), [[7, 64]], 0, 0, False)
+    iota(R("io", 128, 192), [[16, 4], [0, 16]], 0, 0)
+    iota(R("d01"), [[0, 256], [-1, 2]], 1, 0)
+
+    P = col("ci", 0)
+    ms(R("pw", 28, 32, 1, 0, 32), 0)
+    ms(R("fw", 28, 32), 0)
+    for o in (R("bt"), R("et", 256, 512), R("ht"), R("ct"), R("at", 0, 1024), R("at", 1024, 1920)) + tuple(R("pl", 640 * t + 448, 640 * t + 640) for t in range(4)):
+        dma("y", o, R("zz", 0, o[1][0][4] - o[1][0][3]))
+    for c, sh, m in ((2, 0, 15), (3, 4, 1), (4, 5, 3), (5, 4, 7), (6, 0, 3), (7, 0, 31), (8, 0, 1), (9, 1, 3), (10, 3, 1), (11, 1, 1), (12, 5, 1)):
+        ts(col("ci", c), P, sh, A.logical_shift_right, m, A.bitwise_and)
+    ts(col("ci", 13), col("ci", 1), 15, A.bitwise_and)
+    cp(R("cf", 2, 13), R("ci", 2, 13))
+    cI, cE, cQ, cG, c3, cU, c1, cC, cH, cA, cO = [col("cf", c) for c in range(2, 13)]
+    D = lambda c: col("cd", c)
+    ts(col("ci", 15), col("ci", 13), 7.0, A.mult)
+    ts(R("ma", 0, 128), R("j16", 0, 128), cI, A.not_equal, 33792.0, A.mult)
+    ts(col("ci", 14), col("ci", 15), 4, A.logical_shift_right)
+    ts(col("lu", 72), cG, 4.0, A.mult, c3, A.add)
+    ts(D(18), cG, 3.0, A.is_ge)
+    ts(D(7), c1, cE, A.not_equal)
+    ts(D(11), cI, 6.0, A.is_ge, -22.0, A.mult)
+    ts(D(19), cG, 6.0, A.is_ge, D(18), A.add)
+    ts(D(2), cQ, 2.0, A.is_lt, 256.0, A.mult)
+    ts(D(38), cI, 4.0, A.is_lt)
+    ts(D(56), cI, 8.0, A.min)
+    cp(R("cf", 13, 15), R("ci", 13, 15))
+    ms(R("one"), 1.0)
+    lin(D(1), cG, 64.0, 0.0)
+    lin(D(4), cC, 8.0, 0.0)
+    lin(D(3), cG, 131136.0, 2048.0)
+    lin(D(0), cI, -1024.0, 15360.0)
+    lin(D(57), c1, -1.0, 1.0)
+    lin(D(5), cH, 2.0, cE)
+    lin(D(8), cE, -32.0, 160.0)
+    lin(D(10), cC, 8.0, c1)
+    lin(R("m16"), R("ma", 0, 128), 1.0, -32768.0)
+    lin(R("pq", 16, 20), R("iot", 0, 4), 16.0, cI)
+    lin(R("jq", 0, 64), R("iot", 0, 64), 2049.0, D(3))
+    lin(D(6), cC, 32.0, D(5))
+    lin(D(24), cI, -1.0, 2.0)
+    lin(R("jq", 64, 128), R("jq", 0, 64), D(57), 0.0)
+    lin(R("jq", 128, 192), R("jq", 0, 64), c1, 0.0)
+    act(R("wx"), R("iot"))
+    Lexp, Lent, Lexit, Lreo = R("lu", 0, 8), R("lu", 24, 28), R("lu", 32, 34), R("lu", 34, 36)
+    Ls, Lm, Lsm, Ln, La, Lb = R("lu", 36, 39), R("lu", 39, 42), R("lu", 36, 42), R("lu", 48, 51), R("lu", 56, 64), R("lu", 64, 72)
+    ts(R("lu", 16, 20), R("iot", 0, 4), 32.0, A.mult, cI, A.add)
+    ts(Lexp, R("io", 0, 8), D(4), A.add)
+    ts(R("lu", 20, 24), R("lu", 16, 20), 16.0, A.add)
+
+    O = lambda k: R("op", 4 * k, 4 * k + 4)
+    for q in range(4):
+        cp(quad("pall", q, 0, 32), R("pw", 0, 32, 1, 0, 32))
+    cp(R("ff"), R("fw"))
+    cp(R("pq", 0, 16), IND(R("pall"), col("lu", 72)))
+    for k in range(16):
+        q, gq = k // 4, k % 4
+        either(k >= 5, quad("fc", q, 8 * gq, 8 * gq + 8), quad("ff", gq, 8 * q, 8 * q + 8))
+        if k == 0:
+            ts(R("pq", 24, 28), R("pq", 0, 4), D(1), A.subtract)
+            ts(R("pq", 32, 36), R("pq", 0, 4), D(1), A.is_ge)
+            cp(O(8), R("pq", 0, 4))
+            tt(R("pq", 40, 44), R("pq", 24, 28), R("pq", 16, 20), A.subtract)
+        if k == 1:
+            tt(R("pq", 48, 52), R("pq", 40, 44), R("pq", 32, 36), A.mult)
+        if k == 2:
+            tt(R("pq", 56, 60), R("pq", 48, 52), R("pq", 16, 20), A.add)
+        if k == 3:
+            cp(O(0), R("pq", 56, 60))
+    act(R("pa"), IND(R("iot", 0, 64), O(0)))
+    act(R("pb"), IND(R("pa"), O(0)))
+    cp(R("fe"), IND(R("fc"), Lexp))
+    tr(R("ft"), R("fe"))
+
+    V = lambda k: R("sm", 48 * k, 48 * k + 36)
+    V48 = lambda k: R("sm", 48 * k, 48 * k + 48)
+    fill = []
+
+    def later(f, *a):
+        fill.append((f, a))
+
+    def pop(n):
+        for _ in range(n):
+            if fill:
+                f, a = fill.pop(0)
+                f(*a)
+
+    later(ts, col("lu", 34), cH, 2.0, A.mult, D(10), A.add)
+    later(ts, R("mb", 0, 28), R("io", 32, 60), col("cf", 14), A.not_equal, 33792.0, A.mult)
+    later(ts, R("cd", 28, 31), R("iot", 0, 3), D(19), A.is_equal)
+    later(ts, R("ma"), R("j16"), col("cf", 13), A.not_equal, 33792.0, A.mult)
+    later(ts, D(25), D(24), 0.0, A.max, D(22), A.mult)
+    later(ts, La, R("iot", 0, 8), 16.0, A.mult)
+    later(ts, Lb, R("iot", 0, 8), 16.0, A.mult, 1.0, A.add)
+    later(ts, D(39), cI, 1.0, A.add, D(38), A.mult)
+    later(ts, Lexit, R("iot", 0, 2), 4.0, A.mult, D(9), A.add)
+    later(ts, col("lu", 35), D(13), 4.0, A.add, 31.0, A.min)
+    later(cp, R("pl", 1920, 2368), R("xl", 3, 1792, 4))
+    later(qz, R("qu"), R("su"), R("ul"))
+    later(qz, R("q1"), R("s1"), R("one"))
+    later(cp, R("pi", 0, 32), IND(R("pall"), Lreo))
+    later(ts, Lent, R("io", 16, 20), D(56), A.add)
+    later(ts, R("pi", 32, 64), R("pi", 0, 32), 5, A.logical_shift_right, 3, A.bitwise_and)
+    later(ts, R("pi", 64, 96), R("pi", 0, 32), 2, A.logical_shift_right, 96, A.bitwise_and)
+    later(ts, R("pi", 96, 128), R("pi", 0, 32), 31, A.bitwise_and)
+    later(ts, R("pf", 0, 32), R("pi", 32, 64), 128.0, A.mult, 352.0, A.min)
+    later(tt, R("pf", 32, 64), R("pi", 64, 96), R("pi", 96, 128), A.add)
+    later(cp, CAST(R("qua"), dt.uint32), IND(CAST(R("qu"), dt.uint32), La))
+    later(tt, R("pf", 64, 96), R("pf", 0, 32), R("pf", 32, 64), A.add)
+    later(cp, CAST(R("qub"), dt.uint32), IND(CAST(R("qu"), dt.uint32), Lb))
+    later(ts, R("om"), R("pf", 64, 96), 2.0, A.mult, 1.0, A.add)
+    later(ts, R("z8"), R("z7"), 15, A.bitwise_and)
+
+    def on_scalar(l):
+        if l == 0:
+            lin(D(12), cI, 4.0, D(11))
+            lin(D(20), D(19), -3.0, cG)
+            lin(D(9), D(7), D(8), D(6))
+            lin(D(13), c1, -3.0, D(12))
+            lin(D(21), D(20), 4.5, -1.5)
+        if l == 1:
+            lin(D(22), D(21), D(20), 1.0)
+            lin(D(51), cQ, 128.0, -4240.0)
+            lin(D(60), cE, 4096.0, D(0))
+            lin(D(58), D(0), 1.0, -16.0)
+        if l == 2:
+            lin(D(52), D(60), 1.0, 4096.0)
+        if l == 3:
+            lin(D(53), cO, D(51), D(52))
+            lin(D(59), cQ, 128.0, D(58))
+            lin(D(16), col("cf", 14), -1024.0, 6144.0)
+        if 4 <= l <= 6:
+            act(R("pl", 640 * (l - 4), 640 * (l - 4) + 448), R("xl", l - 4, 1792, 4))
+        if l == 8:
+            lin(R("m7", 0, 28), R("mb", 0, 28), 1.0, -32768.0)
+            lin(D(17), col("cf", 13), -1024.0, 15360.0)
+            lin(R("cd", 32, 35), R("cd", 28, 31), D(25), 0.0)
+            lin(R("mk"), R("ma"), 1.0, -32768.0)
+        if l == 9:
+            lin(D(23), D(20), 0.28125, -1.03125)
+            lin(D(36), c1, 2.0, -1.0)
+            lin(D(54), cA, 2.0, -1.0)
+            lin(D(26), D(23), D(20), 1.0)
+            lin(D(37), D(36), -TINY, 0.0)
+            lin(D(55), D(54), -TINY, 0.0)
+            lin(R("mc", 0, 64), R("iot", 0, 64), D(26), -0.46875)
+            lin(D(40), cI, D(38), 0.0)
+            lin(R("cd", 44, 47), R("cd", 28, 31), D(39), -1.0)
+            lin(R("c3", 0, 3), R("iot", 0, 3), 16.0, cI)
+
+    def tables_of_constants():
+        cp(R("zj", 0, 64), R("mc", 0, 64))
+        ts(R("ct", 4 * 144 + 1, 4 * 153, 4), R("iot", 0, 9), cG, A.is_equal, D(40), A.mult)
+        ts(R("zj", 64, 128), R("zj", 0, 64), 3, A.bitwise_and)
+        ts(R("ct", 4 * 153 + 2, 4 * 162, 4), R("iot", 0, 9), cG, A.is_equal, D(40), A.mult)
+        for t, w in ((0, 64), (1, 64), (2, 16)):
+            ts(R("ct", 256 * t, 256 * t + 4 * w, 4), R("zj", 64, 64 + w), D(44 + t), A.is_equal, 262144.0, A.mult)
+        ts(R("c3", 4, 7), R("c3", 0, 3), 35.0, A.min)
+        tt(R("mc", 128, 192), R("z8"), R("io", 128, 192), A.add)
+        qz(R("qc"), R("sc"), R("ct"))
+
+    def constants_for_choosing(k):
+        if k == 0:
+            lin(R("c3", 8, 11), R("c3", 4, 7), 1.0 / 9, -0.444)
+            lin(R("mc", 64, 128), R("iot", 0, 64), -4096.0, 258048.0)
+            lin(R("mc", 192, 256), R("mc", 128, 192), 64.0, 0.0)
+            lin(D(48), cQ, 128.0, cU)
+            ms(R("tt", 64, 320, 80), BIG)
+            ms(R("hh", 64, 240, 80), 0.0)
+            ms(R("dd", 0, 240, 80), 0.0)
+            cp(R("c3i", 0, 3), R("c3", 8, 11))
+            tr(R("pre"), R("v0"))
+            ts(R("c3", 12, 15), R("c3i", 0, 3), 167.0, A.mult, 144.0, A.add)
+            ts(Ln, R("c3i", 0, 3), 3.0, A.mult)
+            tt(R("c3", 16, 19), R("c3", 12, 15), R("c3", 4, 7), A.add)
+            tt(R("hk"), R("mc", 192, 256), R("mc", 64, 128), A.add)
+            for L, c in ((Ls, 0.0), (Lm, 9.0)):
+                ts(L, R("c3", 16, 19), c, A.add)
+        else:
+            lin(D(49), D(48), 2048.0, 2496.0)
+            for ch in range(4):
+                c = 32 * (ch % 2) + 16 * (ch // 2)
+                act(R("sm", 9 * ch, 9 * ch + 9), R("pre", c, c + 9))
+            lin(R("jb", 0, 48), R("io", 64, 112), 2048.0, D(49))
+            lin(R("jb", 64, 112), R("jb", 0, 48), 1.0, 64.0)
+            lin(R("jb", 128, 176), R("jb", 0, 48), 1.0, 128.0)
+
+    O34, OX64, Omid, OX128, O1, O2 = R("op", 28, 30), R("op", 40, 48), R("op", 48, 52), R("op", 56, 64), R("op", 64, 72), R("op", 72, 80)
+
+    def wrap(row, k, n):
+        c = 128 * (k % 2)
+        scan(R("sx", c, c + n), R("m16", 0, n), row, 0.0, A.add, A.max)
+        return lambda a, b: R("sx", c + 16 * a + 15, c + 16 * b, 16)
+
+    def inherit(first, last):
+        steps = [("vb", "v0", 0, "vb"), ("va", "vb", 0, "v0"), ("vb", "va", 1, "vb"), ("va", "vb", 2, "va"), ("vb", "va", 3, "vb"),
+                 ("va", "vb", 4, "va"), ("vz", "va", 5, "vb")]
+        pr = ["pa", "pb"]
+
+        def step(l):
+            o, w, k, i = steps[l]
+            tt(R(o, 16, 80) if o == "vz" else R(o), IND(R(w), O(k)), R(i), A.max)
+
+        if first:
+            for l in range(6):
+                got = wrap(R(pr[(l + 1) % 2] if l < 5 else "pb"), l, 64)
+                if l == 0:
+                    act(R("pa"), IND(R("pb"), O(0)))
+                    act(R("xa"), IND(R("iot"), O(8)))
+                    tt(R("f2", 0, 64), IND(R("ft"), R("lu", 16, 20)), R("jq", 64, 128), A.mult)
+                elif l == 1:
+                    tt(R("v0"), R("f2", 0, 64), R("f2", 64, 128), A.add)
+                    act(R("vb"), R("v0"))
+                else:
+                    step(l - 2)
+                ts(O(l + 1), got(0, 4), D(0), A.subtract)
+                if l < 5:
+                    act(R(pr[(l + 1) % 2]), IND(R(pr[l % 2]), O(l + 1)))
+                if l < 4:
+                    on_scalar(l)
+                if l == 0:
+                    tt(R("f2", 64, 128), IND(R("ft"), R("lu", 20, 24)), R("jq", 128, 192), A.mult)
+                else:
+                    pop(1)
+            act(R("xb"), IND(R("xa"), O(6)))
+            act(R("xz", 0, 64), IND(R("xb"), O(6)))
+            for q in range(4):
+                act(quad("wx", q, 128 * q, 128 * q + 64), quad("xz", q, 0, 64))
+            on_scalar(4)
+            ts(R("pq", 64, 66), got(2, 4), D(58), A.subtract, 48.0, A.is_lt)
+            ts(R("pq", 68, 70), got(2, 4), D(58), A.subtract)
+            step(4)
+            tt(R("pq", 72, 74), R("pq", 64, 66), R("pq", 68, 70), A.mult)
+            tr(R("tx", 0, 64), R("xz", 0, 64))
+            step(5)
+            tr(R("xz", 64, 128), R("tx", 16, 80))
+            cp(O34, R("pq", 72, 74))
+            step(6)
+            got = wrap(R("xz"), 0, 128)
+            pop(1)
+            ts(OX64, got(0, 8), D(0), A.subtract)
+            ts(Omid, got(4, 8), D(59), A.subtract, 0.0, A.max)
+            act(R("xy"), IND(R("wx"), OX64))
+            act(quad("wx", 3, 256, 384), quad("xy", 2, 0, 128))
+        else:
+            for l in range(7):
+                step(l)
+        tt(R("vz", 48, 80), IND(R("vz", 0, 48), O34), R("vz", 48, 80), A.max)
+        if first:
+            pop(1)
+        tr(R("tk", 0, 64), R("vz", 16, 80))
+        if first:
+            got = wrap(R("xy"), 1, 128)
+        tr(R("vz", 80, 144), R("tk", 16, 80))
+        if first:
+            ts(OX128, got(0, 8), D(0), A.subtract)
+            ts(O1, got(0, 8), D(53), A.subtract, 0.0, A.max)
+            act(R("xw"), IND(R("wx"), OX128))
+        tt(R("vz", 80, 144), IND(R("vz", 0, 80), Omid), R("vz", 80, 144), A.max)
+        if first:
+            pop(1)
+        cp(quad("wa", 1, 16, 144), quad("vz", 0, 16, 144))
+        act(quad("wa", 3, 16, 144), quad("vz", 2, 16, 144))
+        act(quad("wb", 2, 0, 128), quad("vz", 0, 16, 144))
+        act(quad("wb", 3, 0, 128), quad("vz", 0, 16, 144))
+        if first:
+            got = wrap(R("xw"), 0, 128)
+        tt(R("l1"), IND(R("wa"), O1), R("vz", 16, 144), A.max)
+        if first:
+            ts(O2, got(0, 8), D(60), A.subtract, D(2), A.max)
+        cp(quad("wb", 2, 128, 256), quad("l1", 1, 0, 128))
+        act(quad("wb", 3, 128, 256), quad("l1", 1, 0, 128))
+        if first:
+            on_scalar(5)
+            on_scalar(6)
+            on_scalar(8)
+            pop(1)
+        tt(R("fin", 16, 144), IND(R("wb"), O2), R("l1"), A.max)
+        if first:
+            pop(1)
+        tr(R("tw", 0, 128), R("fin", 16, 144))
+        tr(R("tw", 128, 288), R("fin"))
+        if first:
+            pop(3)
+        ts(R("pk"), IND(R("tw"), Lexit), 25769803776.0, A.add, 25769803776.0, A.subtract)
+        tt(R("pkf"), IND(R("tw"), Lexit), R("pk"), A.subtract)
+        for k in range(16):
+            q, gq = k // 4, k % 4
+            either(k, quad("hub", gq, 8 * q, 8 * q + 8), quad("pkf", q, 8 * gq, 8 * gq + 8))
+        if last:
+            cp(R("oe", 4, 32), R("hub", 0, 28))
+        else:
+            scan(R("ks", 0, 28), R("m7", 0, 28), R("hub", 0, 28), 0.0, A.add, A.max)
+            cp(R("oe", 4, 36), IND(R("hub"), Lreo))
+            ts(R("oe", 0, 4), R("ks", 6, 28, 7), D(16), A.subtract)
+
+    def gather_e(t, c0, c1, on):
+        either(on, R("et", 512 + 4 * c0 + t, 512 + 4 * c1, 4), IND(R("pl", 640 * t, 640 * t + 640), R("oe", 4 + c0 // 16, 4 + c1 // 16)))
+
+    def pack_e(c0, c1):
+        qz(R("qe", 128 + c0, 128 + c1), R("se", 128 + c0, 128 + c1), R("et", 512 + 4 * c0, 512 + 4 * c1))
+        return R("qe", 128 + c0, 128 + c1), R("se", 128 + c0, 128 + c1)
+
+    inherit(True, False)
+    HALF = ((0, 256), (256, 448))
+
+    for r, h in enumerate(DIST):
+        dst = T.cores[(rank - h) % n_ranks]
+        src = T.cores[(rank + h) % n_ranks]
+        ne = len(topo.engines(src, core))
+        so, lo, qh, sh = "so%d" % r, "lo%d" % r, "qh%d" % r, "sh%d" % r
+        z = 128 - 64 * r
+        note([], R(lo, 0, 12)[1], ("ar%d" % r, ne))
+        note([], R("lq", z, z + 64)[1] + R("ls", z, z + 64)[1], ("ah%d" % r, 2 * ne))
+        count["ar%d" % r], count["ah%d" % r] = ne, 2 * ne
+        for t in range(4):
+            either(t, R("et", t, 256, 4), IND(R("pl", 640 * t, 640 * t + 640), R("oe", 0, 4)))
+        qz(R("qe", 0, 128), R("se", 0, 128), R("et", 0, 512))
+        mm(0, 128, R("qu"), R("su"), R("qe", 0, 128), R("se", 0, 128))
+        for t in range(1, 4):
+            gather_e(t, 0, 256, 1)
+        gather_e(0, 0, 128, 0)
+        for t in range(3):
+            ts(R("bt", 256 * t, 256 * t + 256, 4), PS(0, 0, 64), 0.0, A.is_gt, D(32 + t), A.mult)
+        qz(R("qb"), R("sb"), R("bt"))
+        mm(1, 192, R("q1"), R("s1"), R("qb"), R("sb"))
+        for b in range(4):
+            mm(4 + b, 128, R("qw", 128 * b, 128 * b + 128), R("sw", 128 * b, 128 * b + 128), R("qe", 0, 128), R("se", 0, 128))
+        gather_e(0, 128, 256, 0)
+        scan(R("kc"), R("mk"), PS(1, 0, 192), 0.0, A.add, A.max)
+        ts(R(so, 0, 12), R("kc", 15, 192, 16), D(17), A.subtract)
+        send(T[lo][:, 0:12], R(so, 0, 12), "ar%d" % r, dst)
+        if r == 0:
+            for b in range(4):
+                o = R("dc", 512 * b, 512 * b + 512)
+                run("g", lambda: g.affine_select(o[0], T["one"][:], [[-1, 128], [128, 4]], A.is_equal, 0.0, -128 * b, 1), [R("one")], [o])
+            act(R("sua"), IND(R("su"), La))
+            act(R("sub"), IND(R("su"), Lb))
+            on_scalar(9)
+            qz(R("lq", 192, 320), R("ls", 192, 320), R("ht"))
+            pop(99)
+        for t in range(2, 4):
+            gather_e(t, 256, 448, 1)
+        for k, (c0, c1) in enumerate(HALF):
+            q, s = pack_e(c0, c1)
+            mm(2 * k, c1 - c0, R("qua"), R("sua"), q, s)
+            mm(2 * k + 1, c1 - c0, R("qub"), R("sub"), q, s)
+            if k == 0:
+                gather_e(0, 256, 448, 0)
+                gather_e(1, 256, 448, 0)
+        if r == 0:
+            tables_of_constants()
+        for k, (c0, c1) in enumerate(HALF):
+            if k == 0:
+                act(R("ab", 2 * c0 + 1, 2 * c1, 2), PS(2 * k, 0, c1 - c0), AF.Sign, D(54), D(55))
+            act(R("ab", 2 * c0, 2 * c1, 2), PS(2 * k + 1, 0, c1 - c0), AF.Sign, D(36), D(37))
+        for k, (c0, c1) in enumerate(HALF):
+            if k == 1:
+                ts(R("ab", 2 * c0 + 1, 2 * c1, 2), PS(2 * k, 0, c1 - c0), 0.0, A.is_gt, cA, A.is_equal)
+            scan(R("oh", 2 * c0, 2 * c1), R("d01", 0, 2 * (c1 - c0)), R("ab", 2 * c0, 2 * c1), 0.0, A.max, A.min)
+            act(R("at", 4 * c0 + 1, 4 * c1, 4), R("oh", 2 * c0 + 1, 2 * c1, 2), AF.Relu)
+        for k, (c0, c1) in enumerate(HALF):
+            off = R("om", c0 // 16, c1 // 16)
+            tt(R("at", 4 * c0, 4 * c1, 4), IND(R("oh"), off), R("at", 4 * c0 + 1, 4 * c1, 4), A.max)
+            act(R("at", 4 * c0 + 2, 4 * c1, 4), IND(R("oh"), off), AF.Relu)
+        for b in range(4):
+            act(R("ht", b, 256, 4), PS(4 + b, 0, 64), AF.Copy, 0.03125)
+        for k, (c0, c1) in enumerate(((0, 256), (256, 480))):
+            qz(R("qa", c0, c1), R("sa", c0, c1), R("at", 4 * c0, 4 * c1))
+            for ch in (2 * k, 2 * k + 1):
+                c = (0, 128, 256, 352)[ch]
+                mm(ch, 176, R("qa", c, c + 128), R("sa", c, c + 128), R("qc"), R("sc"))
+        qz(R(qh), R(sh), R("ht"))
+        send(T["lq"][:, z:z + 64].bitcast(dt.uint8), CAST(R(qh, 0, 64), dt.uint8), "ah%d" % r, dst)
+        send(T["ls"][:, z:z + 64], R(sh, 0, 64), "ah%d" % r, dst)
+        if r == 0:
+            constants_for_choosing(0)
+        old, new = V(r % 2), V(1 - r % 2)
+        L = [R(lo, 4 * t, 4 * t + 4) for t in range(3)]
+        W = lambda ch, t: R("tb", 176 * ch + 64 * t, 176 * ch + 64 * t + (64 if t < 2 else 16))
+        for ch in range(4):
+            act(R("tb", 176 * ch, 176 * ch + 176), PS(ch, 0, 176))
+            act(R("g0", 64 * ch, 64 * ch + 64), IND(W(ch, 0), L[0]))
+        act(R("sm", 96, 192), IND(R("tb"), Lsm))
+        if r == 0:
+            constants_for_choosing(1)
+        for t in range(3):
+            tt(R("hh", 80 * t, 80 * t + 64), IND(R("iot", 0, 64), L[t]), R("hk"), A.add)
+        for t in range(3):
+            tt(R("dd", 80 * t + 1, 80 * t + 65), R("hh", 80 * t, 80 * t + 64), R("hh", 80 * t + 1, 80 * t + 65), A.subtract)
+
+        def second(ch):
+            tt(R("g1", 64 * ch, 64 * ch + 64), IND(W(ch, 1), L[1]), R("g0", 64 * ch, 64 * ch + 64), A.add)
+
+        def third(ch):
+            tt(R("tt", 80 * ch, 80 * ch + 64), IND(W(ch, 2), L[2]), R("g1", 64 * ch, 64 * ch + 64), A.add)
+
+        def best(ch):
+            for t in range(3):
+                c = 65 * (3 * ch + t)
+                scan(R("ro", c, c + 65), R("dd", 80 * t, 80 * t + 65), R("tt", 80 * ch, 80 * ch + 65), BIG, A.add, A.max)
+
+        for f, ch in ((second, 0), (second, 1), (third, 0), (third, 1), (best, 0), (second, 2), (best, 1), (second, 3), (third, 2),
+                      (third, 3), (best, 2), (best, 3)):
+            f(ch)
+        cp(R("ri", 0, 12), R("ro", 64, 780, 65))
+        ts(R("ni", 0, 12), R("ri", 0, 12), 6, A.logical_shift_right, 63, A.bitwise_and)
+        for k in range(3):
+            ts(R("fi", k, 36, 3), R("ri", 0, 12), 2 * k, A.logical_shift_right, 3, A.bitwise_and)
+        tt(V48(5), IND(R("ni", 0, 12), Ln), R("jb", 64 * r, 64 * r + 48), A.add)
+        f = R("fi", 0, 36)
+        tt(V(8), f, V(2), A.is_equal)
+        tt(V(6), f, V(2), A.not_equal)
+        tt(V(10), V(8), old, A.mult)
+        tt(V(7), f, V(3), A.not_equal)
+        tt(V(9), V(6), V(5), A.mult)
+        act(R("c1p"), IND(V(10), Lent))
+        tt(V(11), V(9), V(7), A.mult)
+        tt(R("pre"), IND(V(11), Lent), R("c1p"), A.add)
+        tr(R("v0"), R("pre"))
+        tr(R("vb"), R("pre"))
+        if r < 2:
+            tt(new, V(11), V(10), A.add)
+        if r == 1:
+            qz(R("qv"), R("sv"), R("vl"))
+        if r == 2:
+            act(R("fo"), R("v0"), AF.Sign)
+            for k in range(7):
+                dma("y", T.ofl[:, 64 * k:64 * k + 64], R("fo", 0, 64, 1, 16 * k, 16 * k + 8))
+        if r == 0:
+            qz(R("qd"), R("sd"), R("dc"))
+        for b in range(4):
+            mm(4 + b, 128, R("qd", 128 * b, 128 * b + 128), R("sd", 128 * b, 128 * b + 128), R("lq", z, z + 128), R("ls", z, z + 128))
+        for b in range(4):
+            c = 640 * b + 448 + 64 * r
+            act(R("pl", c, c + 64), PS(4 + b, 0, 64))
+        inherit(False, r == 2)
+
+    for half, (c0, c1) in enumerate(((0, 320), (320, 448))):
+        for t in range(4):
+            gather_e(t, c0, c1, t if half == 0 else t > 0)
+        q, s = pack_e(c0, c1)
+        mm(half, c1 - c0, R("qv"), R("sv"), q, s)
+        dma("y", T.oc[:, 4 * c0:4 * c1], CAST(q, dt.uint8))
+    for k in range(4):
+        dma("s" if k % 2 else "y", T.osc[4 * k:4 * k + 4, :], R("se", 128, 576, 1, 32 * k, 32 * k + 4))
+    for half, (c0, c1) in enumerate(((0, 320), (320, 448))):
+        cp(R("yo", c0, c1), PS(half, 0, c1 - c0))
+        dma("y" if half else "s", T.y[:, c0:c1], R("yo", c0, c1))
+    for s, v in count.items():
+        wait("g", (s, v))

@@ -21,7 +21,8 @@ _S = {
     "sx": (256, F32), "op": (80, U16), "om": (32, U16), "pi": (160, I32), "pf": (96, F32),
     "fw": (32, I32), "ff": (32, F32), "fc": (32, F32), "fe": (128, F32), "ft": (128, F32), "f2": (128, F32), "fo": (64, F32), "yo": (448, F32),
     "iot": (448, F32), "ci": (16, I32), "cf": (16, F32), "cd": (64, F32), "j16": (192, F32), "zj": (128, I32),
-    "ma": (192, F32), "mb": (32, F32), "mc": (256, F32), "m16": (128, F32), "mk": (192, F32), "m7": (32, F32), "jq": (192, F32), "hk": (64, F32),
+    "ma": (192, F32), "mz": (128, F32), "mb": (32, F32), "mc": (256, F32), "m16": (128, F32), "mk": (192, F32), "m7": (32, F32),
+    "jq": (192, F32), "hk": (64, F32),
     "jb": (64 * 3, F32), "io": (192, F32), "z7": (64, I32), "z8": (64, I32), "lu": (80, U16), "c3": (48, F32), "c3i": (8, I32),
 }
 SCRATCH = {k: ("sbuf", [128, n], d) for k, (n, d) in _S.items()}
@@ -33,6 +34,7 @@ A = AluOpType
 AF = ActivationFunctionType
 BIG = -4000000.0
 TINY = 2.0 ** -120
+WAKE, FLIGHT, SLACK = 0.22, 2.5, 0.03
 
 
 def rank_program(g, core, T, topo):
@@ -46,13 +48,14 @@ def rank_program(g, core, T, topo):
     waited = {k: {} for k in Q}
     hist = {}
     nd = [0]
+    ops = []
 
     def R(name, c0=0, c1=None, step=1, p0=0, p1=128):
         if c1 is None:
-            c1 = 4096 if name == "ps" else _S[name][0]
+            c1 = _S[name][0]
         ap = T[name][p0:p1, c0:c1:step] if step > 1 else T[name][p0:p1, c0:c1]
         if name == "ps":
-            return (ap, [("ps", 0, 128, c0 // 512 * 512, c0 // 512 * 512 + 512, 1)])
+            return (ap, [("ps", 0, 128, c0 // 512 * 512, c0 // 512 * 512 + 512, 1, c1 - c0)])
         return (ap, [(name, p0, p1, c0, c1, step)])
 
     def IND(w, o):
@@ -71,30 +74,34 @@ def rank_program(g, core, T, topo):
             Q[e].wait_ge(T.sem[tok[0]], tok[1])
             waited[e][tok[0]] = tok[1]
 
-    def deps(e, reads, writes):
-        need = {}
+    def add(e, kind, fn, reads, writes, cost, lat=0.0):
+        before = set()
         for regs, wr in ((reads, False), (writes, True)):
             for r in regs:
-                for (h, tok, hw) in hist.get(r[0], []):
-                    if (wr or hw or (r[0] == "ps" and tok[0] != SEM.get(e))) and meet(r, h):
-                        need[tok[0]] = max(need.get(tok[0], 0), tok[1])
-        for s, v in need.items():
-            wait(e, (s, v))
-
-    def note(reads, writes, tok):
+                for (h, k, hw) in hist.get(r[0], []):
+                    if (wr or hw or (r[0] == "ps" and ops[k][0] != e)) and meet(r, h):
+                        before.add(k)
+        ops.append((e, kind, fn, sorted(before), cost, lat))
         for r in reads:
-            hist.setdefault(r[0], []).append((r, tok, False))
+            hist.setdefault(r[0], []).append((r, len(ops) - 1, False))
         for r in writes:
-            hist.setdefault(r[0], []).append((r, tok, True))
+            hist.setdefault(r[0], []).append((r, len(ops) - 1, True))
 
-    def run(e, fn, ins, outs):
+    def width(v):
+        r = v[1][0]
+        return r[6] if r[0] == "ps" else (r[4] - r[3] + r[5] - 1) // r[5]
+
+    def run(e, fn, ins, outs, per=1.0, fixed=0.0):
         reads = [r for v in ins if isinstance(v, tuple) for r in v[1]]
         writes = [r for v in outs for r in v[1]]
-        deps(e, reads, writes)
-        s = SEM[e]
-        count[s] += 1
-        fn().then_inc(T.sem[s], 1)
-        note(reads, writes, (s, count[s]))
+        n = width(outs[0])
+        if ins and len(ins[0][1]) == 2:
+            cost = 0.055 + n * 0.0013
+        elif fixed:
+            cost = fixed + n * per * 0.001
+        else:
+            cost = max(64, n * per) * 0.001
+        add(e, "c", fn, reads, writes, cost)
 
     def ap(v):
         return v[0] if isinstance(v, tuple) else v
@@ -102,18 +109,52 @@ def rank_program(g, core, T, topo):
     def dma(e, out, in_):
         reads = in_[1] if isinstance(in_, tuple) else []
         writes = out[1] if isinstance(out, tuple) else []
-        deps(e, reads, writes)
-        s = "d%d" % nd[0]
-        nd[0] += 1
-        count[s] = 16
-        Q[e].dma_start(ap(out), ap(in_)).then_inc(T.sem[s], 16)
-        note(reads, writes, (s, 16))
+        v = out if writes else in_
+        add(e, "d", lambda: Q[e].dma_start(ap(out), ap(in_)), reads, writes, 0.06, 2.0 + width(v) * 0.002)
+
+    def issue():
+        n = len(ops)
+        way = [0.0] * n
+        for k in range(n - 1, -1, -1):
+            way[k] += ops[k][4] + ops[k][5]
+            for d in ops[k][3]:
+                way[d] = max(way[d], way[k] + WAKE)
+        start, busy = [0.0] * n, {e: [] for e in Q}
+        for k in sorted(range(n), key=lambda k: (-way[k], k)):
+            e, cost = ops[k][0], ops[k][4]
+            t = max([start[d] + ops[d][4] + ops[d][5] + WAKE for d in ops[k][3]] + [0.0])
+            for (a, b) in busy[e]:
+                if t + cost <= a + SLACK:
+                    break
+                t = max(t, b)
+            start[k] = t
+            busy[e].append((t, t + cost))
+            busy[e].sort()
+        tok = {}
+        for k in sorted(range(n), key=lambda k: (start[k], k)):
+            e, kind, fn = ops[k][:3]
+            need = {}
+            for d in ops[k][3]:
+                need[tok[d][0]] = max(need.get(tok[d][0], 0), tok[d][1])
+            for a, b in need.items():
+                wait(e, (a, b))
+            if kind == "c":
+                count[SEM[e]] += 1
+                tok[k] = (SEM[e], count[SEM[e]])
+                fn().then_inc(T.sem[SEM[e]], 1)
+            elif kind == "d":
+                tok[k] = ("d%d" % nd[0], 16)
+                count[tok[k][0]] = 16
+                nd[0] += 1
+                fn().then_inc(T.sem[tok[k][0]], 16)
+            else:
+                tok[k] = fn()
 
     def cp(o, i):
-        run("v", lambda: g.vector.tensor_copy(o[0], i[0]), [i], [o])
+        run("v", lambda: g.vector.tensor_copy(o[0], i[0]), [i], [o], 0.5 if i[1][0][0] == "xl" else 1.0)
 
     def tt(o, a, b, op):
-        run("v", lambda: g.vector.tensor_tensor(o[0], a[0], b[0], op), [a, b], [o])
+        run("v", lambda: g.vector.tensor_tensor(o[0], a[0], b[0], op), [a, b], [o], 2.0)
 
     def ts(o, a, s1, op0, s2=None, op1=None):
         if op1 is None:
@@ -122,16 +163,16 @@ def rank_program(g, core, T, topo):
             run("v", lambda: g.vector.tensor_scalar(o[0], a[0], ap(s1), ap(s2), op0, op1), [a, s1, s2], [o])
 
     def scan(o, d0, d1, init, op0, op1):
-        run("v", lambda: g.vector.tensor_tensor_scan(o[0], d0[0], d1[0], init, op0, op1), [d0, d1], [o])
+        run("v", lambda: g.vector.tensor_tensor_scan(o[0], d0[0], d1[0], init, op0, op1), [d0, d1], [o], 0.5 if o[1][0][0] == "oh" else 1.0)
 
     def tr(o, i):
         run("v", lambda: g.vector.transpose(o[0], i[0]), [i], [o])
 
     def ms(o, c):
-        run("v", lambda: g.vector.memset(o[0], c), [], [o])
+        run("v", lambda: g.vector.memset(o[0], c), [], [o], 0.5)
 
     def qz(q, s, i):
-        run("v", lambda: g.vector.quantize_mx(q[0], s[0], i[0]), [i], [q, s])
+        run("v", lambda: g.vector.quantize_mx(q[0], s[0], i[0]), [i], [q, s], 0.88, 0.012)
 
     def act(o, i, f=AF.Copy, scale=None, bias=None):
         kw = {}
@@ -146,19 +187,26 @@ def rank_program(g, core, T, topo):
 
     def mm(bank, n, lq, ls, rq, rs):
         o = R("ps", 512 * bank, 512 * bank + n)
-        run("p", lambda: g.tensor.matmul_mx(o[0], lq[0], ls[0], rq[0], rs[0], True, True), [lq, ls, rq, rs], [o])
+        run("p", lambda: g.tensor.matmul_mx(o[0], lq[0], ls[0], rq[0], rs[0], True, True), [lq, ls, rq, rs], [o], 0.83, 0.014)
 
     def iota(o, pat, base, cm, small=True):
         if small:
-            run("g", lambda: g.iota(o[0], pat, base, cm, allow_small_or_imprecise_dtypes=True), [], [o])
+            run("g", lambda: g.iota(o[0], pat, base, cm, allow_small_or_imprecise_dtypes=True), [], [o], 2.0, 0.13)
         else:
-            run("g", lambda: g.iota(o[0], pat, base, cm), [], [o])
+            run("g", lambda: g.iota(o[0], pat, base, cm), [], [o], 2.0, 0.13)
 
-    def send(o, i, sem, dst):
-        deps("g", i[1], [])
-        rid, pid = topo.addr(dst, core)
-        g.remote_dma(o, i[0], T.sem[sem], T.sem["sent"], pid, rid, topo.mask(core, dst))
-        count["sent"] += len(topo.engines(core, dst))
+    def send(o, i, sem, dst, total):
+        def fn():
+            rid, pid = topo.addr(dst, core)
+            g.remote_dma(o[0], i[0], T.sem[sem], T.sem["sent"], pid, rid, topo.mask(core, dst))
+            count["sent"] += len(topo.engines(core, dst))
+            count[sem] = total
+            return (sem, total)
+        add("g", "r", fn, i[1], o[1], 0.5, FLIGHT)
+
+    def unpacker(b):
+        o = R("dc", 512 * b, 512 * b + 512)
+        run("g", lambda: g.affine_select(o[0], T["one"][:], [[-1, 128], [128, 4]], A.is_equal, 0.0, -128 * b, 1), [R("one")], [o], 2.0, 0.17)
 
     def PS(bank, c0, c1):
         return R("ps", 512 * bank + c0, 512 * bank + c1)
@@ -196,6 +244,7 @@ def rank_program(g, core, T, topo):
     iota(R("tk", 64, 80), [[0, 16]], 0, 0)
     iota(R("tx", 64, 80), [[0, 16]], 0, 0)
     iota(R("zz"), [[0, 1024]], 0, 0)
+    iota(R("one"), [[0, 512]], 1, 0)
     iota(R("wa"), [[0, 144]], 0, 0)
     iota(R("wb"), [[0, 272]], 0, 0)
     iota(R("fin"), [[0, 160]], 0, 0)
@@ -203,20 +252,27 @@ def rank_program(g, core, T, topo):
     iota(R("z7"), [[7, 64]], 0, 0, False)
     iota(R("io", 128, 192), [[16, 4], [0, 16]], 0, 0)
     iota(R("d01"), [[0, 256], [-1, 2]], 1, 0)
+    for b in range(4):
+        unpacker(b)
 
     P = col("ci", 0)
     ms(R("pw", 28, 32, 1, 0, 32), 0)
     ms(R("fw", 28, 32), 0)
     for o in (R("bt"), R("et", 256, 512), R("ht"), R("ct"), R("at", 0, 1024), R("at", 1024, 1920)) + tuple(R("pl", 640 * t + 448, 640 * t + 640) for t in range(4)):
-        dma("y", o, R("zz", 0, o[1][0][4] - o[1][0][3]))
+        dma("y", o, R("zz", 0, width(o)))
     for c, sh, m in ((2, 0, 15), (3, 4, 1), (4, 5, 3), (5, 4, 7), (6, 0, 3), (7, 0, 31), (8, 0, 1), (9, 1, 3), (10, 3, 1), (11, 1, 1), (12, 5, 1)):
         ts(col("ci", c), P, sh, A.logical_shift_right, m, A.bitwise_and)
     ts(col("ci", 13), col("ci", 1), 15, A.bitwise_and)
     cp(R("cf", 2, 13), R("ci", 2, 13))
     cI, cE, cQ, cG, c3, cU, c1, cC, cH, cA, cO = [col("cf", c) for c in range(2, 13)]
     D = lambda c: col("cd", c)
+    Lexp, Lent, Lexit, Lreo = R("lu", 0, 8), R("lu", 24, 28), R("lu", 32, 34), R("lu", 34, 36)
+    Ls, Lm, Lsm, Ln, La, Lb = R("lu", 36, 39), R("lu", 39, 42), R("lu", 36, 42), R("lu", 48, 51), R("lu", 56, 64), R("lu", 64, 72)
+    V = lambda k: R("sm", 48 * k, 48 * k + 36)
+    V48 = lambda k: R("sm", 48 * k, 48 * k + 48)
+
     ts(col("ci", 15), col("ci", 13), 7.0, A.mult)
-    ts(R("ma", 0, 128), R("j16", 0, 128), cI, A.not_equal, 33792.0, A.mult)
+    ts(R("mz"), R("j16", 0, 128), cI, A.not_equal, 33792.0, A.mult)
     ts(col("ci", 14), col("ci", 15), 4, A.logical_shift_right)
     ts(col("lu", 72), cG, 4.0, A.mult, c3, A.add)
     ts(D(18), cG, 3.0, A.is_ge)
@@ -227,28 +283,77 @@ def rank_program(g, core, T, topo):
     ts(D(38), cI, 4.0, A.is_lt)
     ts(D(56), cI, 8.0, A.min)
     cp(R("cf", 13, 15), R("ci", 13, 15))
-    ms(R("one"), 1.0)
-    lin(D(1), cG, 64.0, 0.0)
-    lin(D(4), cC, 8.0, 0.0)
-    lin(D(3), cG, 131136.0, 2048.0)
-    lin(D(0), cI, -1024.0, 15360.0)
-    lin(D(57), c1, -1.0, 1.0)
-    lin(D(5), cH, 2.0, cE)
-    lin(D(8), cE, -32.0, 160.0)
-    lin(D(10), cC, 8.0, c1)
-    lin(R("m16"), R("ma", 0, 128), 1.0, -32768.0)
+    for d, i, a, b in ((1, cG, 64.0, 0.0), (4, cC, 8.0, 0.0), (3, cG, 131136.0, 2048.0), (0, cI, -1024.0, 15360.0), (57, c1, -1.0, 1.0),
+                       (5, cH, 2.0, cE), (8, cE, -32.0, 160.0), (10, cC, 8.0, c1), (6, cC, 32.0, D(5)), (24, cI, -1.0, 2.0),
+                       (12, cI, 4.0, D(11)), (20, D(19), -3.0, cG), (9, D(7), D(8), D(6)), (13, c1, -3.0, D(12)), (21, D(20), 4.5, -1.5),
+                       (22, D(21), D(20), 1.0), (51, cQ, 128.0, -4240.0), (60, cE, 4096.0, D(0)), (58, D(0), 1.0, -16.0),
+                       (52, D(60), 1.0, 4096.0), (53, cO, D(51), D(52)), (59, cQ, 128.0, D(58)), (16, col("cf", 14), -1024.0, 6144.0),
+                       (17, col("cf", 13), -1024.0, 15360.0), (23, D(20), 0.28125, -1.03125), (36, c1, 2.0, -1.0), (54, cA, 2.0, -1.0),
+                       (26, D(23), D(20), 1.0), (37, D(36), -TINY, 0.0), (55, D(54), -TINY, 0.0), (40, cI, D(38), 0.0),
+                       (48, cQ, 128.0, cU), (49, D(48), 2048.0, 2496.0), (39, D(40), 1.0, D(38))):
+        lin(D(d), i, a, b)
+    lin(R("m16"), R("mz"), 1.0, -32768.0)
     lin(R("pq", 16, 20), R("iot", 0, 4), 16.0, cI)
     lin(R("jq", 0, 64), R("iot", 0, 64), 2049.0, D(3))
-    lin(D(6), cC, 32.0, D(5))
-    lin(D(24), cI, -1.0, 2.0)
     lin(R("jq", 64, 128), R("jq", 0, 64), D(57), 0.0)
     lin(R("jq", 128, 192), R("jq", 0, 64), c1, 0.0)
     act(R("wx"), R("iot"))
-    Lexp, Lent, Lexit, Lreo = R("lu", 0, 8), R("lu", 24, 28), R("lu", 32, 34), R("lu", 34, 36)
-    Ls, Lm, Lsm, Ln, La, Lb = R("lu", 36, 39), R("lu", 39, 42), R("lu", 36, 42), R("lu", 48, 51), R("lu", 56, 64), R("lu", 64, 72)
     ts(R("lu", 16, 20), R("iot", 0, 4), 32.0, A.mult, cI, A.add)
     ts(Lexp, R("io", 0, 8), D(4), A.add)
     ts(R("lu", 20, 24), R("lu", 16, 20), 16.0, A.add)
+    ts(col("lu", 34), cH, 2.0, A.mult, D(10), A.add)
+    ts(R("mb", 0, 28), R("io", 32, 60), col("cf", 14), A.not_equal, 33792.0, A.mult)
+    ts(R("cd", 28, 31), R("iot", 0, 3), D(19), A.is_equal)
+    ts(R("ma"), R("j16"), col("cf", 13), A.not_equal, 33792.0, A.mult)
+    ts(D(25), D(24), 0.0, A.max, D(22), A.mult)
+    ts(La, R("iot", 0, 8), 16.0, A.mult)
+    ts(Lb, R("iot", 0, 8), 16.0, A.mult, 1.0, A.add)
+    ts(Lexit, R("iot", 0, 2), 4.0, A.mult, D(9), A.add)
+    ts(col("lu", 35), D(13), 4.0, A.add, 31.0, A.min)
+    ts(Lent, R("io", 16, 20), D(56), A.add)
+    ts(R("z8"), R("z7"), 15, A.bitwise_and)
+    lin(R("m7", 0, 28), R("mb", 0, 28), 1.0, -32768.0)
+    lin(R("cd", 32, 35), R("cd", 28, 31), D(25), 0.0)
+    lin(R("mk"), R("ma"), 1.0, -32768.0)
+    lin(R("mc", 0, 64), R("iot", 0, 64), D(26), -0.46875)
+    lin(R("cd", 44, 47), R("cd", 28, 31), D(39), -1.0)
+    lin(R("c3", 0, 3), R("iot", 0, 3), 16.0, cI)
+    cp(R("zj", 0, 64), R("mc", 0, 64))
+    ts(R("ct", 4 * 144 + 1, 4 * 153, 4), R("iot", 0, 9), cG, A.is_equal, D(40), A.mult)
+    ts(R("zj", 64, 128), R("zj", 0, 64), 3, A.bitwise_and)
+    ts(R("ct", 4 * 153 + 2, 4 * 162, 4), R("iot", 0, 9), cG, A.is_equal, D(40), A.mult)
+    for t, w in ((0, 64), (1, 64), (2, 16)):
+        ts(R("ct", 256 * t, 256 * t + 4 * w, 4), R("zj", 64, 64 + w), D(44 + t), A.is_equal, 262144.0, A.mult)
+    ts(R("c3", 4, 7), R("c3", 0, 3), 35.0, A.min)
+    tt(R("mc", 128, 192), R("z8"), R("io", 128, 192), A.add)
+    qz(R("qc"), R("sc"), R("ct"))
+    lin(R("c3", 8, 11), R("c3", 4, 7), 1.0 / 9, -0.444)
+    lin(R("mc", 64, 128), R("iot", 0, 64), -4096.0, 258048.0)
+    lin(R("mc", 192, 256), R("mc", 128, 192), 64.0, 0.0)
+    ms(R("tt", 64, 320, 80), BIG)
+    ms(R("hh", 64, 240, 80), 0.0)
+    ms(R("dd", 0, 240, 80), 0.0)
+    cp(R("c3i", 0, 3), R("c3", 8, 11))
+    ts(R("c3", 12, 15), R("c3i", 0, 3), 167.0, A.mult, 144.0, A.add)
+    ts(Ln, R("c3i", 0, 3), 3.0, A.mult)
+    tt(R("c3", 16, 19), R("c3", 12, 15), R("c3", 4, 7), A.add)
+    tt(R("hk"), R("mc", 192, 256), R("mc", 64, 128), A.add)
+    for L, c in ((Ls, 0.0), (Lm, 9.0)):
+        ts(L, R("c3", 16, 19), c, A.add)
+    lin(R("jb", 0, 48), R("io", 64, 112), 2048.0, D(49))
+    lin(R("jb", 64, 112), R("jb", 0, 48), 1.0, 64.0)
+    lin(R("jb", 128, 176), R("jb", 0, 48), 1.0, 128.0)
+    qz(R("q1"), R("s1"), R("one"))
+    qz(R("qd"), R("sd"), R("dc"))
+    qz(R("lq", 192, 320), R("ls", 192, 320), R("ht"))
+
+    for t in range(4):
+        either(t < 3, R("pl", 640 * t, 640 * t + 448), R("xl", t, 1792, 4))
+    qz(R("qu"), R("su"), R("ul"))
+    qz(R("qv"), R("sv"), R("vl"))
+    for q, s, L in (("qua", "sua", La), ("qub", "sub", Lb)):
+        cp(CAST(R(q), dt.uint32), IND(CAST(R("qu"), dt.uint32), L))
+        act(R(s), IND(R("su"), L))
 
     O = lambda k: R("op", 4 * k, 4 * k + 4)
     for q in range(4):
@@ -258,134 +363,26 @@ def rank_program(g, core, T, topo):
     for k in range(16):
         q, gq = k // 4, k % 4
         either(k >= 5, quad("fc", q, 8 * gq, 8 * gq + 8), quad("ff", gq, 8 * q, 8 * q + 8))
-        if k == 0:
-            ts(R("pq", 24, 28), R("pq", 0, 4), D(1), A.subtract)
-            ts(R("pq", 32, 36), R("pq", 0, 4), D(1), A.is_ge)
-            cp(O(8), R("pq", 0, 4))
-            tt(R("pq", 40, 44), R("pq", 24, 28), R("pq", 16, 20), A.subtract)
-        if k == 1:
-            tt(R("pq", 48, 52), R("pq", 40, 44), R("pq", 32, 36), A.mult)
-        if k == 2:
-            tt(R("pq", 56, 60), R("pq", 48, 52), R("pq", 16, 20), A.add)
-        if k == 3:
-            cp(O(0), R("pq", 56, 60))
+    ts(R("pq", 24, 28), R("pq", 0, 4), D(1), A.subtract)
+    ts(R("pq", 32, 36), R("pq", 0, 4), D(1), A.is_ge)
+    cp(O(8), R("pq", 0, 4))
+    tt(R("pq", 40, 44), R("pq", 24, 28), R("pq", 32, 36), A.mult)
+    ts(R("pq", 76, 80), R("pq", 0, 4), D(1), A.is_lt)
+    tt(R("pq", 48, 52), R("pq", 76, 80), R("pq", 16, 20), A.mult)
+    tt(R("pq", 56, 60), R("pq", 48, 52), R("pq", 40, 44), A.add)
+    cp(O(0), R("pq", 56, 60))
     act(R("pa"), IND(R("iot", 0, 64), O(0)))
     act(R("pb"), IND(R("pa"), O(0)))
     cp(R("fe"), IND(R("fc"), Lexp))
     tr(R("ft"), R("fe"))
-
-    V = lambda k: R("sm", 48 * k, 48 * k + 36)
-    V48 = lambda k: R("sm", 48 * k, 48 * k + 48)
-    fill = []
-
-    def later(f, *a):
-        fill.append((f, a))
-
-    def pop(n):
-        for _ in range(n):
-            if fill:
-                f, a = fill.pop(0)
-                f(*a)
-
-    later(ts, col("lu", 34), cH, 2.0, A.mult, D(10), A.add)
-    later(ts, R("mb", 0, 28), R("io", 32, 60), col("cf", 14), A.not_equal, 33792.0, A.mult)
-    later(ts, R("cd", 28, 31), R("iot", 0, 3), D(19), A.is_equal)
-    later(ts, R("ma"), R("j16"), col("cf", 13), A.not_equal, 33792.0, A.mult)
-    later(ts, D(25), D(24), 0.0, A.max, D(22), A.mult)
-    later(ts, La, R("iot", 0, 8), 16.0, A.mult)
-    later(ts, Lb, R("iot", 0, 8), 16.0, A.mult, 1.0, A.add)
-    later(ts, D(39), cI, 1.0, A.add, D(38), A.mult)
-    later(ts, Lexit, R("iot", 0, 2), 4.0, A.mult, D(9), A.add)
-    later(ts, col("lu", 35), D(13), 4.0, A.add, 31.0, A.min)
-    later(cp, R("pl", 1920, 2368), R("xl", 3, 1792, 4))
-    later(qz, R("qu"), R("su"), R("ul"))
-    later(qz, R("q1"), R("s1"), R("one"))
-    later(cp, R("pi", 0, 32), IND(R("pall"), Lreo))
-    later(ts, Lent, R("io", 16, 20), D(56), A.add)
-    later(ts, R("pi", 32, 64), R("pi", 0, 32), 5, A.logical_shift_right, 3, A.bitwise_and)
-    later(ts, R("pi", 64, 96), R("pi", 0, 32), 2, A.logical_shift_right, 96, A.bitwise_and)
-    later(ts, R("pi", 96, 128), R("pi", 0, 32), 31, A.bitwise_and)
-    later(ts, R("pf", 0, 32), R("pi", 32, 64), 128.0, A.mult, 352.0, A.min)
-    later(tt, R("pf", 32, 64), R("pi", 64, 96), R("pi", 96, 128), A.add)
-    later(cp, CAST(R("qua"), dt.uint32), IND(CAST(R("qu"), dt.uint32), La))
-    later(tt, R("pf", 64, 96), R("pf", 0, 32), R("pf", 32, 64), A.add)
-    later(cp, CAST(R("qub"), dt.uint32), IND(CAST(R("qu"), dt.uint32), Lb))
-    later(ts, R("om"), R("pf", 64, 96), 2.0, A.mult, 1.0, A.add)
-    later(ts, R("z8"), R("z7"), 15, A.bitwise_and)
-
-    def on_scalar(l):
-        if l == 0:
-            lin(D(12), cI, 4.0, D(11))
-            lin(D(20), D(19), -3.0, cG)
-            lin(D(9), D(7), D(8), D(6))
-            lin(D(13), c1, -3.0, D(12))
-            lin(D(21), D(20), 4.5, -1.5)
-        if l == 1:
-            lin(D(22), D(21), D(20), 1.0)
-            lin(D(51), cQ, 128.0, -4240.0)
-            lin(D(60), cE, 4096.0, D(0))
-            lin(D(58), D(0), 1.0, -16.0)
-        if l == 2:
-            lin(D(52), D(60), 1.0, 4096.0)
-        if l == 3:
-            lin(D(53), cO, D(51), D(52))
-            lin(D(59), cQ, 128.0, D(58))
-            lin(D(16), col("cf", 14), -1024.0, 6144.0)
-        if 4 <= l <= 6:
-            act(R("pl", 640 * (l - 4), 640 * (l - 4) + 448), R("xl", l - 4, 1792, 4))
-        if l == 8:
-            lin(R("m7", 0, 28), R("mb", 0, 28), 1.0, -32768.0)
-            lin(D(17), col("cf", 13), -1024.0, 15360.0)
-            lin(R("cd", 32, 35), R("cd", 28, 31), D(25), 0.0)
-            lin(R("mk"), R("ma"), 1.0, -32768.0)
-        if l == 9:
-            lin(D(23), D(20), 0.28125, -1.03125)
-            lin(D(36), c1, 2.0, -1.0)
-            lin(D(54), cA, 2.0, -1.0)
-            lin(D(26), D(23), D(20), 1.0)
-            lin(D(37), D(36), -TINY, 0.0)
-            lin(D(55), D(54), -TINY, 0.0)
-            lin(R("mc", 0, 64), R("iot", 0, 64), D(26), -0.46875)
-            lin(D(40), cI, D(38), 0.0)
-            lin(R("cd", 44, 47), R("cd", 28, 31), D(39), -1.0)
-            lin(R("c3", 0, 3), R("iot", 0, 3), 16.0, cI)
-
-    def tables_of_constants():
-        cp(R("zj", 0, 64), R("mc", 0, 64))
-        ts(R("ct", 4 * 144 + 1, 4 * 153, 4), R("iot", 0, 9), cG, A.is_equal, D(40), A.mult)
-        ts(R("zj", 64, 128), R("zj", 0, 64), 3, A.bitwise_and)
-        ts(R("ct", 4 * 153 + 2, 4 * 162, 4), R("iot", 0, 9), cG, A.is_equal, D(40), A.mult)
-        for t, w in ((0, 64), (1, 64), (2, 16)):
-            ts(R("ct", 256 * t, 256 * t + 4 * w, 4), R("zj", 64, 64 + w), D(44 + t), A.is_equal, 262144.0, A.mult)
-        ts(R("c3", 4, 7), R("c3", 0, 3), 35.0, A.min)
-        tt(R("mc", 128, 192), R("z8"), R("io", 128, 192), A.add)
-        qz(R("qc"), R("sc"), R("ct"))
-
-    def constants_for_choosing(k):
-        if k == 0:
-            lin(R("c3", 8, 11), R("c3", 4, 7), 1.0 / 9, -0.444)
-            lin(R("mc", 64, 128), R("iot", 0, 64), -4096.0, 258048.0)
-            lin(R("mc", 192, 256), R("mc", 128, 192), 64.0, 0.0)
-            lin(D(48), cQ, 128.0, cU)
-            ms(R("tt", 64, 320, 80), BIG)
-            ms(R("hh", 64, 240, 80), 0.0)
-            ms(R("dd", 0, 240, 80), 0.0)
-            cp(R("c3i", 0, 3), R("c3", 8, 11))
-            tr(R("pre"), R("v0"))
-            ts(R("c3", 12, 15), R("c3i", 0, 3), 167.0, A.mult, 144.0, A.add)
-            ts(Ln, R("c3i", 0, 3), 3.0, A.mult)
-            tt(R("c3", 16, 19), R("c3", 12, 15), R("c3", 4, 7), A.add)
-            tt(R("hk"), R("mc", 192, 256), R("mc", 64, 128), A.add)
-            for L, c in ((Ls, 0.0), (Lm, 9.0)):
-                ts(L, R("c3", 16, 19), c, A.add)
-        else:
-            lin(D(49), D(48), 2048.0, 2496.0)
-            for ch in range(4):
-                c = 32 * (ch % 2) + 16 * (ch // 2)
-                act(R("sm", 9 * ch, 9 * ch + 9), R("pre", c, c + 9))
-            lin(R("jb", 0, 48), R("io", 64, 112), 2048.0, D(49))
-            lin(R("jb", 64, 112), R("jb", 0, 48), 1.0, 64.0)
-            lin(R("jb", 128, 176), R("jb", 0, 48), 1.0, 128.0)
+    cp(R("pi", 0, 32), IND(R("pall"), Lreo))
+    ts(R("pi", 32, 64), R("pi", 0, 32), 5, A.logical_shift_right, 3, A.bitwise_and)
+    ts(R("pi", 64, 96), R("pi", 0, 32), 2, A.logical_shift_right, 96, A.bitwise_and)
+    ts(R("pi", 96, 128), R("pi", 0, 32), 31, A.bitwise_and)
+    ts(R("pf", 0, 32), R("pi", 32, 64), 128.0, A.mult, 352.0, A.min)
+    tt(R("pf", 32, 64), R("pi", 64, 96), R("pi", 96, 128), A.add)
+    tt(R("pf", 64, 96), R("pf", 0, 32), R("pf", 32, 64), A.add)
+    ts(R("om"), R("pf", 64, 96), 2.0, A.mult, 1.0, A.add)
 
     O34, OX64, Omid, OX128, O1, O2 = R("op", 28, 30), R("op", 40, 48), R("op", 48, 52), R("op", 56, 64), R("op", 64, 72), R("op", 72, 80)
 
@@ -394,96 +391,64 @@ def rank_program(g, core, T, topo):
         scan(R("sx", c, c + n), R("m16", 0, n), row, 0.0, A.add, A.max)
         return lambda a, b: R("sx", c + 16 * a + 15, c + 16 * b, 16)
 
-    def inherit(first, last):
-        steps = [("vb", "v0", 0, "vb"), ("va", "vb", 0, "v0"), ("vb", "va", 1, "vb"), ("va", "vb", 2, "va"), ("vb", "va", 3, "vb"),
-                 ("va", "vb", 4, "va"), ("vz", "va", 5, "vb")]
-        pr = ["pa", "pb"]
+    pr = ["pa", "pb"]
+    for l in range(6):
+        got = wrap(R(pr[(l + 1) % 2] if l < 5 else "pb"), l, 64)
+        if l == 0:
+            act(R("pa"), IND(R("pb"), O(0)))
+            act(R("xa"), IND(R("iot"), O(8)))
+        ts(O(l + 1), got(0, 4), D(0), A.subtract)
+        if l < 5:
+            act(R(pr[(l + 1) % 2]), IND(R(pr[l % 2]), O(l + 1)))
+    act(R("xb"), IND(R("xa"), O(6)))
+    act(R("xz", 0, 64), IND(R("xb"), O(6)))
+    for q in range(4):
+        act(quad("wx", q, 128 * q, 128 * q + 64), quad("xz", q, 0, 64))
+    ts(R("pq", 64, 66), got(2, 4), D(58), A.subtract, 48.0, A.is_lt)
+    ts(R("pq", 68, 70), got(2, 4), D(58), A.subtract)
+    tt(R("pq", 72, 74), R("pq", 64, 66), R("pq", 68, 70), A.mult)
+    cp(O34, R("pq", 72, 74))
+    tr(R("tx", 0, 64), R("xz", 0, 64))
+    tr(R("xz", 64, 128), R("tx", 16, 80))
+    got = wrap(R("xz"), 0, 128)
+    ts(OX64, got(0, 8), D(0), A.subtract)
+    ts(Omid, got(4, 8), D(59), A.subtract, 0.0, A.max)
+    act(R("xy"), IND(R("wx"), OX64))
+    act(quad("wx", 3, 256, 384), quad("xy", 2, 0, 128))
+    got = wrap(R("xy"), 1, 128)
+    ts(OX128, got(0, 8), D(0), A.subtract)
+    ts(O1, got(0, 8), D(53), A.subtract, 0.0, A.max)
+    act(R("xw"), IND(R("wx"), OX128))
+    got = wrap(R("xw"), 0, 128)
+    ts(O2, got(0, 8), D(60), A.subtract, D(2), A.max)
 
-        def step(l):
-            o, w, k, i = steps[l]
+    tt(R("f2", 0, 64), IND(R("ft"), R("lu", 16, 20)), R("jq", 64, 128), A.mult)
+    tt(R("f2", 64, 128), IND(R("ft"), R("lu", 20, 24)), R("jq", 128, 192), A.mult)
+    tt(R("v0"), R("f2", 0, 64), R("f2", 64, 128), A.add)
+    tt(R("vb"), R("f2", 0, 64), R("f2", 64, 128), A.add)
+    tr(R("pre"), R("v0"))
+    for ch in range(4):
+        c = 32 * (ch % 2) + 16 * (ch // 2)
+        act(R("sm", 9 * ch, 9 * ch + 9), R("pre", c, c + 9))
+
+    def inherit(last):
+        for o, w, k, i in (("vb", "v0", 0, "vb"), ("va", "vb", 0, "v0"), ("vb", "va", 1, "vb"), ("va", "vb", 2, "va"), ("vb", "va", 3, "vb"),
+                           ("va", "vb", 4, "va"), ("vz", "va", 5, "vb")):
             tt(R(o, 16, 80) if o == "vz" else R(o), IND(R(w), O(k)), R(i), A.max)
-
-        if first:
-            for l in range(6):
-                got = wrap(R(pr[(l + 1) % 2] if l < 5 else "pb"), l, 64)
-                if l == 0:
-                    act(R("pa"), IND(R("pb"), O(0)))
-                    act(R("xa"), IND(R("iot"), O(8)))
-                    tt(R("f2", 0, 64), IND(R("ft"), R("lu", 16, 20)), R("jq", 64, 128), A.mult)
-                elif l == 1:
-                    tt(R("v0"), R("f2", 0, 64), R("f2", 64, 128), A.add)
-                    act(R("vb"), R("v0"))
-                else:
-                    step(l - 2)
-                ts(O(l + 1), got(0, 4), D(0), A.subtract)
-                if l < 5:
-                    act(R(pr[(l + 1) % 2]), IND(R(pr[l % 2]), O(l + 1)))
-                if l < 4:
-                    on_scalar(l)
-                if l == 0:
-                    tt(R("f2", 64, 128), IND(R("ft"), R("lu", 20, 24)), R("jq", 128, 192), A.mult)
-                else:
-                    pop(1)
-            act(R("xb"), IND(R("xa"), O(6)))
-            act(R("xz", 0, 64), IND(R("xb"), O(6)))
-            for q in range(4):
-                act(quad("wx", q, 128 * q, 128 * q + 64), quad("xz", q, 0, 64))
-            on_scalar(4)
-            ts(R("pq", 64, 66), got(2, 4), D(58), A.subtract, 48.0, A.is_lt)
-            ts(R("pq", 68, 70), got(2, 4), D(58), A.subtract)
-            step(4)
-            tt(R("pq", 72, 74), R("pq", 64, 66), R("pq", 68, 70), A.mult)
-            tr(R("tx", 0, 64), R("xz", 0, 64))
-            step(5)
-            tr(R("xz", 64, 128), R("tx", 16, 80))
-            cp(O34, R("pq", 72, 74))
-            step(6)
-            got = wrap(R("xz"), 0, 128)
-            pop(1)
-            ts(OX64, got(0, 8), D(0), A.subtract)
-            ts(Omid, got(4, 8), D(59), A.subtract, 0.0, A.max)
-            act(R("xy"), IND(R("wx"), OX64))
-            act(quad("wx", 3, 256, 384), quad("xy", 2, 0, 128))
-        else:
-            for l in range(7):
-                step(l)
         tt(R("vz", 48, 80), IND(R("vz", 0, 48), O34), R("vz", 48, 80), A.max)
-        if first:
-            pop(1)
         tr(R("tk", 0, 64), R("vz", 16, 80))
-        if first:
-            got = wrap(R("xy"), 1, 128)
         tr(R("vz", 80, 144), R("tk", 16, 80))
-        if first:
-            ts(OX128, got(0, 8), D(0), A.subtract)
-            ts(O1, got(0, 8), D(53), A.subtract, 0.0, A.max)
-            act(R("xw"), IND(R("wx"), OX128))
         tt(R("vz", 80, 144), IND(R("vz", 0, 80), Omid), R("vz", 80, 144), A.max)
-        if first:
-            pop(1)
         cp(quad("wa", 1, 16, 144), quad("vz", 0, 16, 144))
         act(quad("wa", 3, 16, 144), quad("vz", 2, 16, 144))
         act(quad("wb", 2, 0, 128), quad("vz", 0, 16, 144))
         act(quad("wb", 3, 0, 128), quad("vz", 0, 16, 144))
-        if first:
-            got = wrap(R("xw"), 0, 128)
         tt(R("l1"), IND(R("wa"), O1), R("vz", 16, 144), A.max)
-        if first:
-            ts(O2, got(0, 8), D(60), A.subtract, D(2), A.max)
         cp(quad("wb", 2, 128, 256), quad("l1", 1, 0, 128))
         act(quad("wb", 3, 128, 256), quad("l1", 1, 0, 128))
-        if first:
-            on_scalar(5)
-            on_scalar(6)
-            on_scalar(8)
-            pop(1)
         tt(R("fin", 16, 144), IND(R("wb"), O2), R("l1"), A.max)
-        if first:
-            pop(1)
         tr(R("tw", 0, 128), R("fin", 16, 144))
         tr(R("tw", 128, 288), R("fin"))
-        if first:
-            pop(3)
         ts(R("pk"), IND(R("tw"), Lexit), 25769803776.0, A.add, 25769803776.0, A.subtract)
         tt(R("pkf"), IND(R("tw"), Lexit), R("pk"), A.subtract)
         for k in range(16):
@@ -503,7 +468,7 @@ def rank_program(g, core, T, topo):
         qz(R("qe", 128 + c0, 128 + c1), R("se", 128 + c0, 128 + c1), R("et", 512 + 4 * c0, 512 + 4 * c1))
         return R("qe", 128 + c0, 128 + c1), R("se", 128 + c0, 128 + c1)
 
-    inherit(True, False)
+    inherit(False)
     HALF = ((0, 256), (256, 448))
 
     for r, h in enumerate(DIST):
@@ -512,71 +477,50 @@ def rank_program(g, core, T, topo):
         ne = len(topo.engines(src, core))
         so, lo, qh, sh = "so%d" % r, "lo%d" % r, "qh%d" % r, "sh%d" % r
         z = 128 - 64 * r
-        note([], R(lo, 0, 12)[1], ("ar%d" % r, ne))
-        note([], R("lq", z, z + 64)[1] + R("ls", z, z + 64)[1], ("ah%d" % r, 2 * ne))
-        count["ar%d" % r], count["ah%d" % r] = ne, 2 * ne
         for t in range(4):
             either(t, R("et", t, 256, 4), IND(R("pl", 640 * t, 640 * t + 640), R("oe", 0, 4)))
         qz(R("qe", 0, 128), R("se", 0, 128), R("et", 0, 512))
         mm(0, 128, R("qu"), R("su"), R("qe", 0, 128), R("se", 0, 128))
-        for t in range(1, 4):
-            gather_e(t, 0, 256, 1)
-        gather_e(0, 0, 128, 0)
         for t in range(3):
             ts(R("bt", 256 * t, 256 * t + 256, 4), PS(0, 0, 64), 0.0, A.is_gt, D(32 + t), A.mult)
         qz(R("qb"), R("sb"), R("bt"))
         mm(1, 192, R("q1"), R("s1"), R("qb"), R("sb"))
-        for b in range(4):
-            mm(4 + b, 128, R("qw", 128 * b, 128 * b + 128), R("sw", 128 * b, 128 * b + 128), R("qe", 0, 128), R("se", 0, 128))
-        gather_e(0, 128, 256, 0)
         scan(R("kc"), R("mk"), PS(1, 0, 192), 0.0, A.add, A.max)
         ts(R(so, 0, 12), R("kc", 15, 192, 16), D(17), A.subtract)
-        send(T[lo][:, 0:12], R(so, 0, 12), "ar%d" % r, dst)
-        if r == 0:
-            for b in range(4):
-                o = R("dc", 512 * b, 512 * b + 512)
-                run("g", lambda: g.affine_select(o[0], T["one"][:], [[-1, 128], [128, 4]], A.is_equal, 0.0, -128 * b, 1), [R("one")], [o])
-            act(R("sua"), IND(R("su"), La))
-            act(R("sub"), IND(R("su"), Lb))
-            on_scalar(9)
-            qz(R("lq", 192, 320), R("ls", 192, 320), R("ht"))
-            pop(99)
-        for t in range(2, 4):
-            gather_e(t, 256, 448, 1)
+        send(R(lo, 0, 12), R(so, 0, 12), "ar%d" % r, dst, ne)
+        for b in range(4):
+            mm(4 + b, 128, R("qw", 128 * b, 128 * b + 128), R("sw", 128 * b, 128 * b + 128), R("qe", 0, 128), R("se", 0, 128))
+            act(R("ht", b, 256, 4), PS(4 + b, 0, 64), AF.Copy, 0.03125)
+        qz(R(qh), R(sh), R("ht"))
+        send(CAST(R("lq", z, z + 64), dt.uint8), CAST(R(qh, 0, 64), dt.uint8), "ah%d" % r, dst, 2 * ne)
+        send(R("ls", z, z + 64), R(sh, 0, 64), "ah%d" % r, dst, 2 * ne)
+        for t in range(1, 4):
+            gather_e(t, 0, 256, 1)
+        gather_e(0, 0, 128, 0)
+        gather_e(0, 128, 256, 0)
+        for t in range(4):
+            gather_e(t, 256, 448, t > 1)
         for k, (c0, c1) in enumerate(HALF):
             q, s = pack_e(c0, c1)
-            mm(2 * k, c1 - c0, R("qua"), R("sua"), q, s)
-            mm(2 * k + 1, c1 - c0, R("qub"), R("sub"), q, s)
+            ba, bb = ((2, 3), (0, 1))[k]
+            mm(ba, c1 - c0, R("qua"), R("sua"), q, s)
+            mm(bb, c1 - c0, R("qub"), R("sub"), q, s)
             if k == 0:
-                gather_e(0, 256, 448, 0)
-                gather_e(1, 256, 448, 0)
-        if r == 0:
-            tables_of_constants()
-        for k, (c0, c1) in enumerate(HALF):
-            if k == 0:
-                act(R("ab", 2 * c0 + 1, 2 * c1, 2), PS(2 * k, 0, c1 - c0), AF.Sign, D(54), D(55))
-            act(R("ab", 2 * c0, 2 * c1, 2), PS(2 * k + 1, 0, c1 - c0), AF.Sign, D(36), D(37))
-        for k, (c0, c1) in enumerate(HALF):
-            if k == 1:
-                ts(R("ab", 2 * c0 + 1, 2 * c1, 2), PS(2 * k, 0, c1 - c0), 0.0, A.is_gt, cA, A.is_equal)
+                act(R("ab", 2 * c0 + 1, 2 * c1, 2), PS(ba, 0, c1 - c0), AF.Sign, D(54), D(55))
+            else:
+                ts(R("ab", 2 * c0 + 1, 2 * c1, 2), PS(ba, 0, c1 - c0), 0.0, A.is_gt, cA, A.is_equal)
+            act(R("ab", 2 * c0, 2 * c1, 2), PS(bb, 0, c1 - c0), AF.Sign, D(36), D(37))
             scan(R("oh", 2 * c0, 2 * c1), R("d01", 0, 2 * (c1 - c0)), R("ab", 2 * c0, 2 * c1), 0.0, A.max, A.min)
             act(R("at", 4 * c0 + 1, 4 * c1, 4), R("oh", 2 * c0 + 1, 2 * c1, 2), AF.Relu)
         for k, (c0, c1) in enumerate(HALF):
             off = R("om", c0 // 16, c1 // 16)
             tt(R("at", 4 * c0, 4 * c1, 4), IND(R("oh"), off), R("at", 4 * c0 + 1, 4 * c1, 4), A.max)
             act(R("at", 4 * c0 + 2, 4 * c1, 4), IND(R("oh"), off), AF.Relu)
-        for b in range(4):
-            act(R("ht", b, 256, 4), PS(4 + b, 0, 64), AF.Copy, 0.03125)
         for k, (c0, c1) in enumerate(((0, 256), (256, 480))):
             qz(R("qa", c0, c1), R("sa", c0, c1), R("at", 4 * c0, 4 * c1))
             for ch in (2 * k, 2 * k + 1):
                 c = (0, 128, 256, 352)[ch]
                 mm(ch, 176, R("qa", c, c + 128), R("sa", c, c + 128), R("qc"), R("sc"))
-        qz(R(qh), R(sh), R("ht"))
-        send(T["lq"][:, z:z + 64].bitcast(dt.uint8), CAST(R(qh, 0, 64), dt.uint8), "ah%d" % r, dst)
-        send(T["ls"][:, z:z + 64], R(sh, 0, 64), "ah%d" % r, dst)
-        if r == 0:
-            constants_for_choosing(0)
         old, new = V(r % 2), V(1 - r % 2)
         L = [R(lo, 4 * t, 4 * t + 4) for t in range(3)]
         W = lambda ch, t: R("tb", 176 * ch + 64 * t, 176 * ch + 64 * t + (64 if t < 2 else 16))
@@ -584,27 +528,15 @@ def rank_program(g, core, T, topo):
             act(R("tb", 176 * ch, 176 * ch + 176), PS(ch, 0, 176))
             act(R("g0", 64 * ch, 64 * ch + 64), IND(W(ch, 0), L[0]))
         act(R("sm", 96, 192), IND(R("tb"), Lsm))
-        if r == 0:
-            constants_for_choosing(1)
         for t in range(3):
             tt(R("hh", 80 * t, 80 * t + 64), IND(R("iot", 0, 64), L[t]), R("hk"), A.add)
-        for t in range(3):
             tt(R("dd", 80 * t + 1, 80 * t + 65), R("hh", 80 * t, 80 * t + 64), R("hh", 80 * t + 1, 80 * t + 65), A.subtract)
-
-        def second(ch):
+        for ch in range(4):
             tt(R("g1", 64 * ch, 64 * ch + 64), IND(W(ch, 1), L[1]), R("g0", 64 * ch, 64 * ch + 64), A.add)
-
-        def third(ch):
             tt(R("tt", 80 * ch, 80 * ch + 64), IND(W(ch, 2), L[2]), R("g1", 64 * ch, 64 * ch + 64), A.add)
-
-        def best(ch):
             for t in range(3):
                 c = 65 * (3 * ch + t)
                 scan(R("ro", c, c + 65), R("dd", 80 * t, 80 * t + 65), R("tt", 80 * ch, 80 * ch + 65), BIG, A.add, A.max)
-
-        for f, ch in ((second, 0), (second, 1), (third, 0), (third, 1), (best, 0), (second, 2), (best, 1), (second, 3), (third, 2),
-                      (third, 3), (best, 2), (best, 3)):
-            f(ch)
         cp(R("ri", 0, 12), R("ro", 64, 780, 65))
         ts(R("ni", 0, 12), R("ri", 0, 12), 6, A.logical_shift_right, 63, A.bitwise_and)
         for k in range(3):
@@ -623,20 +555,15 @@ def rank_program(g, core, T, topo):
         tr(R("vb"), R("pre"))
         if r < 2:
             tt(new, V(11), V(10), A.add)
-        if r == 1:
-            qz(R("qv"), R("sv"), R("vl"))
-        if r == 2:
+        else:
             act(R("fo"), R("v0"), AF.Sign)
             for k in range(7):
                 dma("y", T.ofl[:, 64 * k:64 * k + 64], R("fo", 0, 64, 1, 16 * k, 16 * k + 8))
-        if r == 0:
-            qz(R("qd"), R("sd"), R("dc"))
         for b in range(4):
             mm(4 + b, 128, R("qd", 128 * b, 128 * b + 128), R("sd", 128 * b, 128 * b + 128), R("lq", z, z + 128), R("ls", z, z + 128))
-        for b in range(4):
             c = 640 * b + 448 + 64 * r
             act(R("pl", c, c + 64), PS(4 + b, 0, 64))
-        inherit(False, r == 2)
+        inherit(r == 2)
 
     for half, (c0, c1) in enumerate(((0, 320), (320, 448))):
         for t in range(4):
@@ -644,10 +571,10 @@ def rank_program(g, core, T, topo):
         q, s = pack_e(c0, c1)
         mm(half, c1 - c0, R("qv"), R("sv"), q, s)
         dma("y", T.oc[:, 4 * c0:4 * c1], CAST(q, dt.uint8))
-    for k in range(4):
-        dma("s" if k % 2 else "y", T.osc[4 * k:4 * k + 4, :], R("se", 128, 576, 1, 32 * k, 32 * k + 4))
-    for half, (c0, c1) in enumerate(((0, 320), (320, 448))):
         cp(R("yo", c0, c1), PS(half, 0, c1 - c0))
         dma("y" if half else "s", T.y[:, c0:c1], R("yo", c0, c1))
+    for k in range(4):
+        dma("s" if k % 2 else "y", T.osc[4 * k:4 * k + 4, :], R("se", 128, 576, 1, 32 * k, 32 * k + 4))
+    issue()
     for s, v in count.items():
         wait("g", (s, v))

from concourse.mybir import dt, AluOpType, ActivationFunctionType

F32, BF, I32, U16, X4, U8 = "float32", "bfloat16", "int32", "uint16", "float8_e4m3fn_x4", "uint8"
_S = {
    "xl": (1792, BF), "pl": (2560, BF), "ul": (512, BF), "vl": (512, BF), "zz": (1024, BF),
    "qu": (128, X4), "su": (128, U8), "qua": (128, X4), "sua": (128, U8), "qub": (128, X4), "sub": (128, U8),
    "qv": (128, X4), "sv": (128, U8), "qw": (512, X4), "sw": (512, U8),
    "et": (2304, BF), "qe": (576, X4), "se": (576, U8), "bt": (768, BF), "qb": (192, X4), "sb": (192, U8),
    "ht": (512, BF), "qh0": (128, X4), "sh0": (128, U8), "qh1": (128, X4), "sh1": (128, U8), "qh2": (128, X4), "sh2": (128, U8),
    "lq": (320, X4), "ls": (320, U8), "ab": (896, BF), "oh": (896, BF), "d01": (512, BF),
    "at": (1920, BF), "qa": (480, X4), "sa": (480, U8), "ct": (704, BF), "qc": (176, X4), "sc": (176, U8),
    "dc": (2048, BF), "qd": (512, X4), "sd": (512, U8), "one": (512, BF), "q1": (128, X4), "s1": (128, U8),
    "tb": (704, F32), "so0": (16, U16), "so1": (16, U16), "so2": (16, U16), "lo0": (16, U16), "lo1": (16, U16), "lo2": (16, U16),
    "kc": (192, F32), "g0": (256, F32), "g1": (256, F32), "tt": (320, F32), "hh": (240, F32), "dd": (240, F32), "ro": (780, F32),
    "ri": (16, I32), "fi": (48, I32), "ni": (16, I32), "sm": (48 * 12, F32),
    "pre": (64, F32), "c1p": (64, F32), "va": (64, F32), "vb": (64, F32), "v0": (64, F32), "vz": (144, F32), "tk": (80, F32),
    "wa": (144, F32), "wb": (272, F32), "wx": (448, F32), "l1": (128, F32), "fin": (160, F32), "tw": (288, F32),
    "pk": (32, F32), "pkf": (32, F32), "hub": (32, F32), "ks": (32, F32),
    "oe": (36, U16), "pw": (32, I32), "pall": (32, F32), "pq": (96, F32), "pa": (64, F32), "pb": (64, F32), "xa": (64, F32),
    "xb": (64, F32), "xz": (128, F32), "xy": (128, F32), "xw": (128, F32), "tx": (80, F32),
    "sx": (256, F32), "op": (80, U16), "om": (32, U16), "pi": (160, I32), "pf": (96, F32),
    "fw": (32, I32), "ff": (32, F32), "fc": (32, F32), "fe": (128, F32), "ft": (128, F32), "f2": (128, F32), "fo": (64, F32), "yo": (448, F32),
    "iot": (448, F32), "ci": (16, I32), "cf": (16, F32), "cd": (64, F32), "j16": (192, F32), "zj": (128, I32),
    "ma": (192, F32), "mz": (128, F32), "mb": (32, F32), "mc": (256, F32), "m16": (128, F32), "mk": (192, F32), "m7": (32, F32),
    "jq": (192, F32), "hk": (64, F32),
    "jb": (64 * 3, F32), "io": (192, F32), "z7": (64, I32), "z8": (64, I32), "lu": (80, U16), "c3": (48, F32), "c3i": (8, I32),
}
SCRATCH = {k: ("sbuf", [128, n], d) for k, (n, d) in _S.items()}
SCRATCH["ps"] = ("psum", [128, 4096], F32)
SEMAPHORES = ["cv", "cs", "cp", "cg", "sent"] + ["d%d" % k for k in range(44)] + ["ar0", "ar1", "ar2", "ah0", "ah1", "ah2"]

DIST = [1, 2, 4]
A = AluOpType
AF = ActivationFunctionType
BIG = -4000000.0
TINY = 2.0 ** -120
WAKE, FLIGHT, SLACK = 0.22, 2.5, 0.03


def rank_program(g, core, T, topo):
    rank = T.rank_of(core)
    if rank is None:
        return
    n_ranks = len(T.cores)
    Q = {"v": g.vector, "s": g.scalar, "p": g.tensor, "g": g, "y": g.sync}
    SEM = {"v": "cv", "s": "cs", "p": "cp", "g": "cg"}
    count = {"cv": 0, "cs": 0, "cp": 0, "cg": 0, "sent": 0}
    waited = {k: {} for k in Q}
    hist = {}
    nd = [0]
    ops = []

    def R(name, c0=0, c1=None, step=1, p0=0, p1=128):
        if c1 is None:
            c1 = _S[name][0]
        ap = T[name][p0:p1, c0:c1:step] if step > 1 else T[name][p0:p1, c0:c1]
        if name == "ps":
            return (ap, [("ps", 0, 128, c0 // 512 * 512, c0 // 512 * 512 + 512, 1, c1 - c0)])
        return (ap, [(name, p0, p1, c0, c1, step)])

    def IND(w, o):
        return (w[0].indirect(o[0]), w[1] + o[1])

    def CAST(v, d):
        return (v[0].bitcast(d), v[1])

    def meet(a, b):
        if a[1] >= b[2] or b[1] >= a[2] or a[3] >= b[4] or b[3] >= a[4]:
            return False
        return not (a[5] == b[5] and a[5] > 1 and (a[3] - b[3]) % a[5])

    def wait(e, tok):
        if waited[e].get(tok[0], 0) < tok[1]:
            Q[e].wait_ge(T.sem[tok[0]], tok[1])
            waited[e][tok[0]] = tok[1]

    def add(e, kind, fn, reads, writes, cost, lat=0.0):
        before = set()
        for regs, wr in ((reads, False), (writes, True)):
            for r in regs:
                for (h, k, hw) in hist.get(r[0], []):
                    if (wr or hw or (r[0] == "ps" and ops[k][0] != e)) and meet(r, h):
                        before.add(k)
        ops.append((e, kind, fn, sorted(before), cost, lat))
        for r in reads:
            hist.setdefault(r[0], []).append((r, len(ops) - 1, False))
        for r in writes:
            hist.setdefault(r[0], []).append((r, len(ops) - 1, True))

    def width(v):
        r = v[1][0]
        return r[6] if r[0] == "ps" else (r[4] - r[3] + r[5] - 1) // r[5]

    def run(e, fn, ins, outs, per=1.0, fixed=0.0):
        reads = [r for v in ins if isinstance(v, tuple) for r in v[1]]
        writes = [r for v in outs for r in v[1]]
        n = width(outs[0])
        if ins and len(ins[0][1]) == 2:
            cost = 0.055 + n * 0.0013
        elif fixed:
            cost = fixed + n * per * 0.001
        else:
            cost = max(64, n * per) * 0.001
        add(e, "c", fn, reads, writes, cost)

    def ap(v):
        return v[0] if isinstance(v, tuple) else v

    def dma(e, out, in_):
        reads = in_[1] if isinstance(in_, tuple) else []
        writes = out[1] if isinstance(out, tuple) else []
        v = out if writes else in_
        add(e, "d", lambda: Q[e].dma_start(ap(out), ap(in_)), reads, writes, 0.06, 2.0 + width(v) * 0.002)

    def issue():
        n = len(ops)
        way = [0.0] * n
        for k in range(n - 1, -1, -1):
            way[k] += ops[k][4] + ops[k][5]
            for d in ops[k][3]:
                way[d] = max(way[d], way[k] + WAKE)
        start, busy = [0.0] * n, {e: [] for e in Q}
        for k in sorted(range(n), key=lambda k: (-way[k], k)):
            e, cost = ops[k][0], ops[k][4]
            t = max([start[d] + ops[d][4] + ops[d][5] + WAKE for d in ops[k][3]] + [0.0])
            for (a, b) in busy[e]:
                if t + cost <= a + SLACK:
                    break
                t = max(t, b)
            start[k] = t
            busy[e].append((t, t + cost))
            busy[e].sort()
        tok = {}
        for k in sorted(range(n), key=lambda k: (start[k], k)):
            e, kind, fn = ops[k][:3]
            need = {}
            for d in ops[k][3]:
                need[tok[d][0]] = max(need.get(tok[d][0], 0), tok[d][1])
            for a, b in need.items():
                wait(e, (a, b))
            if kind == "c":
                count[SEM[e]] += 1
                tok[k] = (SEM[e], count[SEM[e]])
                fn().then_inc(T.sem[SEM[e]], 1)
            elif kind == "d":
                tok[k] = ("d%d" % nd[0], 16)
                count[tok[k][0]] = 16
                nd[0] += 1
                fn().then_inc(T.sem[tok[k][0]], 16)
            else:
                tok[k] = fn()

    def cp(o, i):
        run("v", lambda: g.vector.tensor_copy(o[0], i[0]), [i], [o], 0.5 if i[1][0][0] == "xl" else 1.0)

    def tt(o, a, b, op):
        run("v", lambda: g.vector.tensor_tensor(o[0], a[0], b[0], op), [a, b], [o], 2.0)

    def ts(o, a, s1, op0, s2=None, op1=None):
        if op1 is None:
            run("v", lambda: g.vector.tensor_scalar(o[0], a[0], ap(s1), None, op0), [a, s1], [o])
        else:
            run("v", lambda: g.vector.tensor_scalar(o[0], a[0], ap(s1), ap(s2), op0, op1), [a, s1, s2], [o])

    def scan(o, d0, d1, init, op0, op1):
        run("v", lambda: g.vector.tensor_tensor_scan(o[0], d0[0], d1[0], init, op0, op1), [d0, d1], [o], 0.5 if o[1][0][0] == "oh" else 1.0)

    def tr(o, i):
        run("v", lambda: g.vector.transpose(o[0], i[0]), [i], [o])

    def ms(o, c):
        run("v", lambda: g.vector.memset(o[0], c), [], [o], 0.5)

    def qz(q, s, i):
        run("v", lambda: g.vector.quantize_mx(q[0], s[0], i[0]), [i], [q, s], 0.88, 0.012)

    def act(o, i, f=AF.Copy, scale=None, bias=None):
        kw = {}
        if scale is not None:
            kw["scale"] = ap(scale)
        if bias is not None:
            kw["bias"] = ap(bias)
        run("s", lambda: g.scalar.activation(o[0], i[0], f, **kw), [i, scale, bias], [o])

    def lin(o, i, scale, bias):
        act(o, i, AF.Identity, scale, bias)

    def mm(bank, n, lq, ls, rq, rs):
        o = R("ps", 512 * bank, 512 * bank + n)
        run("p", lambda: g.tensor.matmul_mx(o[0], lq[0], ls[0], rq[0], rs[0], True, True), [lq, ls, rq, rs], [o], 0.83, 0.014)

    def iota(o, pat, base, cm, small=True):
        if small:
            run("g", lambda: g.iota(o[0], pat, base, cm, allow_small_or_imprecise_dtypes=True), [], [o], 2.0, 0.13)
        else:
            run("g", lambda: g.iota(o[0], pat, base, cm), [], [o], 2.0, 0.13)

    def send(o, i, sem, dst, total):
        def fn():
            rid, pid = topo.addr(dst, core)
            g.remote_dma(o[0], i[0], T.sem[sem], T.sem["sent"], pid, rid, topo.mask(core, dst))
            count["sent"] += len(topo.engines(core, dst))
            count[sem] = total
            return (sem, total)
        add("g", "r", fn, i[1], o[1], 0.5, FLIGHT)

    def unpacker(b):
        o = R("dc", 512 * b, 512 * b + 512)
        run("g", lambda: g.affine_select(o[0], T["one"][:], [[-1, 128], [128, 4]], A.is_equal, 0.0, -128 * b, 1), [R("one")], [o], 2.0, 0.17)

    def PS(bank, c0, c1):
        return R("ps", 512 * bank + c0, 512 * bank + c1)

    def col(name, c):
        return R(name, c, c + 1)

    def quad(name, q, c0, c1, step=1):
        return R(name, c0, c1, step, 32 * q, 32 * q + 32)

    def either(k, o, i):
        if k % 2:
            act(o, i)
        else:
            cp(o, i)

    dma("y", R("pw", 0, 28, 1, 0, 16), T.par[:])
    dma("s", R("pw", 0, 28, 1, 16, 32), T.par[:])
    dma("y", R("fw", 0, 28), T.fl[:])
    dma("s", R("xl", 0, 896), T.x[:, 0:896])
    dma("y", R("xl", 896, 1792), T.x[:, 896:1792])
    dma("y", R("ul"), T.u[:])
    dma("y", CAST(R("qw"), dt.uint8), T.wc[:])
    dma("y", R("sw"), T.ws[:])
    dma("y", R("vl"), T.v[:])

    iota(col("ci", 0), [[0, 1]], 0, 1, False)
    iota(col("ci", 1), [[0, 1]], 0, 7, False)
    iota(R("j16"), [[0, 12], [1, 16]], 0, 0)
    iota(R("iot"), [[1, 448]], 0, 0)
    iota(R("io", 0, 8), [[2, 2], [1, 2], [4, 2]], 0, 0)
    iota(R("io", 16, 20), [[9, 2], [18, 2]], 0, 0)
    iota(R("io", 32, 60), [[0, 4], [1, 7]], 0, 0)
    iota(R("vz", 0, 16), [[0, 16]], 0, 0)
    iota(R("tk", 64, 80), [[0, 16]], 0, 0)
    iota(R("tx", 64, 80), [[0, 16]], 0, 0)
    iota(R("zz"), [[0, 1024]], 0, 0)
    iota(R("one"), [[0, 512]], 1, 0)
    iota(R("wa"), [[0, 144]], 0, 0)
    iota(R("wb"), [[0, 272]], 0, 0)
    iota(R("fin"), [[0, 160]], 0, 0)
    iota(R("io", 64, 118), [[32, 6], [0, 9]], 0, 0)
    iota(R("z7"), [[7, 64]], 0, 0, False)
    iota(R("io", 128, 192), [[16, 4], [0, 16]], 0, 0)
    iota(R("d01"), [[0, 256], [-1, 2]], 1, 0)
    for b in range(4):
        unpacker(b)

    P = col("ci", 0)
    ms(R("pw", 28, 32, 1, 0, 32), 0)
    ms(R("fw", 28, 32), 0)
    for o in (R("bt"), R("et", 256, 512), R("ht"), R("ct"), R("at", 0, 1024), R("at", 1024, 1920)) + tuple(R("pl", 640 * t + 448, 640 * t + 640) for t in range(4)):
        dma("y", o, R("zz", 0, width(o)))
    for c, sh, m in ((2, 0, 15), (3, 4, 1), (4, 5, 3), (5, 4, 7), (6, 0, 3), (7, 0, 31), (8, 0, 1), (9, 1, 3), (10, 3, 1), (11, 1, 1), (12, 5, 1)):
        ts(col("ci", c), P, sh, A.logical_shift_right, m, A.bitwise_and)
    ts(col("ci", 13), col("ci", 1), 15, A.bitwise_and)
    cp(R("cf", 2, 13), R("ci", 2, 13))
    cI, cE, cQ, cG, c3, cU, c1, cC, cH, cA, cO = [col("cf", c) for c in range(2, 13)]
    D = lambda c: col("cd", c)
    Lexp, Lent, Lexit, Lreo = R("lu", 0, 8), R("lu", 24, 28), R("lu", 32, 34), R("lu", 34, 36)
    Ls, Lm, Lsm, Ln, La, Lb = R("lu", 36, 39), R("lu", 39, 42), R("lu", 36, 42), R("lu", 48, 51), R("lu", 56, 64), R("lu", 64, 72)
    V = lambda k: R("sm", 48 * k, 48 * k + 36)
    V48 = lambda k: R("sm", 48 * k, 48 * k + 48)

    ts(col("ci", 15), col("ci", 13), 7.0, A.mult)
    ts(R("mz"), R("j16", 0, 128), cI, A.not_equal, 33792.0, A.mult)
    ts(col("ci", 14), col("ci", 15), 4, A.logical_shift_right)
    ts(col("lu", 72), cG, 4.0, A.mult, c3, A.add)
    ts(D(18), cG, 3.0, A.is_ge)
    ts(D(7), c1, cE, A.not_equal)
    ts(D(11), cI, 6.0, A.is_ge, -22.0, A.mult)
    ts(D(19), cG, 6.0, A.is_ge, D(18), A.add)
    ts(D(2), cQ, 2.0, A.is_lt, 256.0, A.mult)
    ts(D(38), cI, 4.0, A.is_lt)
    ts(D(56), cI, 8.0, A.min)
    cp(R("cf", 13, 15), R("ci", 13, 15))
    for d, i, a, b in ((1, cG, 64.0, 0.0), (4, cC, 8.0, 0.0), (3, cG, 131136.0, 2048.0), (0, cI, -1024.0, 15360.0), (57, c1, -1.0, 1.0),
                       (5, cH, 2.0, cE), (8, cE, -32.0, 160.0), (10, cC, 8.0, c1), (6, cC, 32.0, D(5)), (24, cI, -1.0, 2.0),
                       (12, cI, 4.0, D(11)), (20, D(19), -3.0, cG), (9, D(7), D(8), D(6)), (13, c1, -3.0, D(12)), (21, D(20), 4.5, -1.5),
                       (22, D(21), D(20), 1.0), (51, cQ, 128.0, -4240.0), (60, cE, 4096.0, D(0)), (58, D(0), 1.0, -16.0),
                       (52, D(60), 1.0, 4096.0), (53, cO, D(51), D(52)), (59, cQ, 128.0, D(58)), (16, col("cf", 14), -1024.0, 6144.0),
                       (17, col("cf", 13), -1024.0, 15360.0), (23, D(20), 0.28125, -1.03125), (36, c1, 2.0, -1.0), (54, cA, 2.0, -1.0),
                       (26, D(23), D(20), 1.0), (37, D(36), -TINY, 0.0), (55, D(54), -TINY, 0.0), (40, cI, D(38), 0.0),
                       (48, cQ, 128.0, cU), (49, D(48), 2048.0, 2496.0), (39, D(40), 1.0, D(38))):
        lin(D(d), i, a, b)
    lin(R("m16"), R("mz"), 1.0, -32768.0)
    lin(R("pq", 16, 20), R("iot", 0, 4), 16.0, cI)
    lin(R("jq", 0, 64), R("iot", 0, 64), 2049.0, D(3))
    lin(R("jq", 64, 128), R("jq", 0, 64), D(57), 0.0)
    lin(R("jq", 128, 192), R("jq", 0, 64), c1, 0.0)
    act(R("wx"), R("iot"))
    ts(R("lu", 16, 20), R("iot", 0, 4), 32.0, A.mult, cI, A.add)
    ts(Lexp, R("io", 0, 8), D(4), A.add)
    ts(R("lu", 20, 24), R("lu", 16, 20), 16.0, A.add)
    ts(col("lu", 34), cH, 2.0, A.mult, D(10), A.add)
    ts(R("mb", 0, 28), R("io", 32, 60), col("cf", 14), A.not_equal, 33792.0, A.mult)
    ts(R("cd", 28, 31), R("iot", 0, 3), D(19), A.is_equal)
    ts(R("ma"), R("j16"), col("cf", 13), A.not_equal, 33792.0, A.mult)
    ts(D(25), D(24), 0.0, A.max, D(22), A.mult)
    ts(La, R("iot", 0, 8), 16.0, A.mult)
    ts(Lb, R("iot", 0, 8), 16.0, A.mult, 1.0, A.add)
    ts(Lexit, R("iot", 0, 2), 4.0, A.mult, D(9), A.add)
    ts(col("lu", 35), D(13), 4.0, A.add, 31.0, A.min)
    ts(Lent, R("io", 16, 20), D(56), A.add)
    ts(R("z8"), R("z7"), 15, A.bitwise_and)
    lin(R("m7", 0, 28), R("mb", 0, 28), 1.0, -32768.0)
    lin(R("cd", 32, 35), R("cd", 28, 31), D(25), 0.0)
    lin(R("mk"), R("ma"), 1.0, -32768.0)
    lin(R("mc", 0, 64), R("iot", 0, 64), D(26), -0.46875)
    lin(R("cd", 44, 47), R("cd", 28, 31), D(39), -1.0)
    lin(R("c3", 0, 3), R("iot", 0, 3), 16.0, cI)
    cp(R("zj", 0, 64), R("mc", 0, 64))
    ts(R("ct", 4 * 144 + 1, 4 * 153, 4), R("iot", 0, 9), cG, A.is_equal, D(40), A.mult)
    ts(R("zj", 64, 128), R("zj", 0, 64), 3, A.bitwise_and)
    ts(R("ct", 4 * 153 + 2, 4 * 162, 4), R("iot", 0, 9), cG, A.is_equal, D(40), A.mult)
    for t, w in ((0, 64), (1, 64), (2, 16)):
        ts(R("ct", 256 * t, 256 * t + 4 * w, 4), R("zj", 64, 64 + w), D(44 + t), A.is_equal, 262144.0, A.mult)
    ts(R("c3", 4, 7), R("c3", 0, 3), 35.0, A.min)
    tt(R("mc", 128, 192), R("z8"), R("io", 128, 192), A.add)
    qz(R("qc"), R("sc"), R("ct"))
    lin(R("c3", 8, 11), R("c3", 4, 7), 1.0 / 9, -0.444)
    lin(R("mc", 64, 128), R("iot", 0, 64), -4096.0, 258048.0)
    lin(R("mc", 192, 256), R("mc", 128, 192), 64.0, 0.0)
    ms(R("tt", 64, 320, 80), BIG)
    ms(R("hh", 64, 240, 80), 0.0)
    ms(R("dd", 0, 240, 80), 0.0)
    cp(R("c3i", 0, 3), R("c3", 8, 11))
    ts(R("c3", 12, 15), R("c3i", 0, 3), 167.0, A.mult, 144.0, A.add)
    ts(Ln, R("c3i", 0, 3), 3.0, A.mult)
    tt(R("c3", 16, 19), R("c3", 12, 15), R("c3", 4, 7), A.add)
    tt(R("hk"), R("mc", 192, 256), R("mc", 64, 128), A.add)
    for L, c in ((Ls, 0.0), (Lm, 9.0)):
        ts(L, R("c3", 16, 19), c, A.add)
    lin(R("jb", 0, 48), R("io", 64, 112), 2048.0, D(49))
    lin(R("jb", 64, 112), R("jb", 0, 48), 1.0, 64.0)
    lin(R("jb", 128, 176), R("jb", 0, 48), 1.0, 128.0)
    qz(R("q1"), R("s1"), R("one"))
    qz(R("qd"), R("sd"), R("dc"))
    qz(R("lq", 192, 320), R("ls", 192, 320), R("ht"))

    for t in range(4):
        either(t < 3, R("pl", 640 * t, 640 * t + 448), R("xl", t, 1792, 4))
    qz(R("qu"), R("su"), R("ul"))
    qz(R("qv"), R("sv"), R("vl"))
    for q, s, L in (("qua", "sua", La), ("qub", "sub", Lb)):
        cp(CAST(R(q), dt.uint32), IND(CAST(R("qu"), dt.uint32), L))
        act(R(s), IND(R("su"), L))

    O = lambda k: R("op", 4 * k, 4 * k + 4)
    for q in range(4):
        cp(quad("pall", q, 0, 32), R("pw", 0, 32, 1, 0, 32))
    cp(R("ff"), R("fw"))
    cp(R("pq", 0, 16), IND(R("pall"), col("lu", 72)))
    for k in range(16):
        q, gq = k // 4, k % 4
        either(k >= 5, quad("fc", q, 8 * gq, 8 * gq + 8), quad("ff", gq, 8 * q, 8 * q + 8))
    ts(R("pq", 24, 28), R("pq", 0, 4), D(1), A.subtract)
    ts(R("pq", 32, 36), R("pq", 0, 4), D(1), A.is_ge)
    cp(O(8), R("pq", 0, 4))
    tt(R("pq", 40, 44), R("pq", 24, 28), R("pq", 32, 36), A.mult)
    ts(R("pq", 76, 80), R("pq", 0, 4), D(1), A.is_lt)
    tt(R("pq", 48, 52), R("pq", 76, 80), R("pq", 16, 20), A.mult)
    tt(R("pq", 56, 60), R("pq", 48, 52), R("pq", 40, 44), A.add)
    cp(O(0), R("pq", 56, 60))
    act(R("pa"), IND(R("iot", 0, 64), O(0)))
    act(R("pb"), IND(R("pa"), O(0)))
    cp(R("fe"), IND(R("fc"), Lexp))
    tr(R("ft"), R("fe"))
    cp(R("pi", 0, 32), IND(R("pall"), Lreo))
    ts(R("pi", 32, 64), R("pi", 0, 32), 5, A.logical_shift_right, 3, A.bitwise_and)
    ts(R("pi", 64, 96), R("pi", 0, 32), 2, A.logical_shift_right, 96, A.bitwise_and)
    ts(R("pi", 96, 128), R("pi", 0, 32), 31, A.bitwise_and)
    ts(R("pf", 0, 32), R("pi", 32, 64), 128.0, A.mult, 352.0, A.min)
    tt(R("pf", 32, 64), R("pi", 64, 96), R("pi", 96, 128), A.add)
    tt(R("pf", 64, 96), R("pf", 0, 32), R("pf", 32, 64), A.add)
    ts(R("om"), R("pf", 64, 96), 2.0, A.mult, 1.0, A.add)

    O34, OX64, Omid, OX128, O1, O2 = R("op", 28, 30), R("op", 40, 48), R("op", 48, 52), R("op", 56, 64), R("op", 64, 72), R("op", 72, 80)

    def wrap(row, k, n):
        c = 128 * (k % 2)
        scan(R("sx", c, c + n), R("m16", 0, n), row, 0.0, A.add, A.max)
        return lambda a, b: R("sx", c + 16 * a + 15, c + 16 * b, 16)

    pr = ["pa", "pb"]
    for l in range(6):
        got = wrap(R(pr[(l + 1) % 2] if l < 5 else "pb"), l, 64)
        if l == 0:
            act(R("pa"), IND(R("pb"), O(0)))
            act(R("xa"), IND(R("iot"), O(8)))
        ts(O(l + 1), got(0, 4), D(0), A.subtract)
        if l < 5:
            act(R(pr[(l + 1) % 2]), IND(R(pr[l % 2]), O(l + 1)))
    act(R("xb"), IND(R("xa"), O(6)))
    act(R("xz", 0, 64), IND(R("xb"), O(6)))
    for q in range(4):
        act(quad("wx", q, 128 * q, 128 * q + 64), quad("xz", q, 0, 64))
    ts(R("pq", 64, 66), got(2, 4), D(58), A.subtract, 48.0, A.is_lt)
    ts(R("pq", 68, 70), got(2, 4), D(58), A.subtract)
    tt(R("pq", 72, 74), R("pq", 64, 66), R("pq", 68, 70), A.mult)
    cp(O34, R("pq", 72, 74))
    tr(R("tx", 0, 64), R("xz", 0, 64))
    tr(R("xz", 64, 128), R("tx", 16, 80))
    got = wrap(R("xz"), 0, 128)
    ts(OX64, got(0, 8), D(0), A.subtract)
    ts(Omid, got(4, 8), D(59), A.subtract, 0.0, A.max)
    act(R("xy"), IND(R("wx"), OX64))
    act(quad("wx", 3, 256, 384), quad("xy", 2, 0, 128))
    got = wrap(R("xy"), 1, 128)
    ts(OX128, got(0, 8), D(0), A.subtract)
    ts(O1, got(0, 8), D(53), A.subtract, 0.0, A.max)
    act(R("xw"), IND(R("wx"), OX128))
    got = wrap(R("xw"), 0, 128)
    ts(O2, got(0, 8), D(60), A.subtract, D(2), A.max)

    tt(R("f2", 0, 64), IND(R("ft"), R("lu", 16, 20)), R("jq", 64, 128), A.mult)
    tt(R("f2", 64, 128), IND(R("ft"), R("lu", 20, 24)), R("jq", 128, 192), A.mult)
    tt(R("v0"), R("f2", 0, 64), R("f2", 64, 128), A.add)
    tt(R("vb"), R("f2", 0, 64), R("f2", 64, 128), A.add)
    tr(R("pre"), R("v0"))
    for ch in range(4):
        c = 32 * (ch % 2) + 16 * (ch // 2)
        act(R("sm", 9 * ch, 9 * ch + 9), R("pre", c, c + 9))

    def inherit(last):
        for o, w, k, i in (("vb", "v0", 0, "vb"), ("va", "vb", 0, "v0"), ("vb", "va", 1, "vb"), ("va", "vb", 2, "va"), ("vb", "va", 3, "vb"),
                           ("va", "vb", 4, "va"), ("vz", "va", 5, "vb")):
            tt(R(o, 16, 80) if o == "vz" else R(o), IND(R(w), O(k)), R(i), A.max)
        tt(R("vz", 48, 80), IND(R("vz", 0, 48), O34), R("vz", 48, 80), A.max)
        tr(R("tk", 0, 64), R("vz", 16, 80))
        tr(R("vz", 80, 144), R("tk", 16, 80))
        tt(R("vz", 80, 144), IND(R("vz", 0, 80), Omid), R("vz", 80, 144), A.max)
        cp(quad("wa", 1, 16, 144), quad("vz", 0, 16, 144))
        act(quad("wa", 3, 16, 144), quad("vz", 2, 16, 144))
        act(quad("wb", 2, 0, 128), quad("vz", 0, 16, 144))
        act(quad("wb", 3, 0, 128), quad("vz", 0, 16, 144))
        tt(R("l1"), IND(R("wa"), O1), R("vz", 16, 144), A.max)
        cp(quad("wb", 2, 128, 256), quad("l1", 1, 0, 128))
        act(quad("wb", 3, 128, 256), quad("l1", 1, 0, 128))
        tt(R("fin", 16, 144), IND(R("wb"), O2), R("l1"), A.max)
        tr(R("tw", 0, 128), R("fin", 16, 144))
        tr(R("tw", 128, 288), R("fin"))
        ts(R("pk"), IND(R("tw"), Lexit), 25769803776.0, A.add, 25769803776.0, A.subtract)
        tt(R("pkf"), IND(R("tw"), Lexit), R("pk"), A.subtract)
        for k in range(16):
            q, gq = k // 4, k % 4
            either(k, quad("hub", gq, 8 * q, 8 * q + 8), quad("pkf", q, 8 * gq, 8 * gq + 8))
        if last:
            cp(R("oe", 4, 32), R("hub", 0, 28))
        else:
            scan(R("ks", 0, 28), R("m7", 0, 28), R("hub", 0, 28), 0.0, A.add, A.max)
            cp(R("oe", 4, 36), IND(R("hub"), Lreo))
            ts(R("oe", 0, 4), R("ks", 6, 28, 7), D(16), A.subtract)

    def gather_e(t, c0, c1, on):
        either(on, R("et", 512 + 4 * c0 + t, 512 + 4 * c1, 4), IND(R("pl", 640 * t, 640 * t + 640), R("oe", 4 + c0 // 16, 4 + c1 // 16)))

    def pack_e(c0, c1):
        qz(R("qe", 128 + c0, 128 + c1), R("se", 128 + c0, 128 + c1), R("et", 512 + 4 * c0, 512 + 4 * c1))
        return R("qe", 128 + c0, 128 + c1), R("se", 128 + c0, 128 + c1)

    inherit(False)
    HALF = ((0, 256), (256, 448))

    for r, h in enumerate(DIST):
        dst = T.cores[(rank - h) % n_ranks]
        src = T.cores[(rank + h) % n_ranks]
        ne = len(topo.engines(src, core))
        so, lo, qh, sh = "so%d" % r, "lo%d" % r, "qh%d" % r, "sh%d" % r
        z = 128 - 64 * r
        for t in range(4):
            either(t, R("et", t, 256, 4), IND(R("pl", 640 * t, 640 * t + 640), R("oe", 0, 4)))
        qz(R("qe", 0, 128), R("se", 0, 128), R("et", 0, 512))
        mm(0, 128, R("qu"), R("su"), R("qe", 0, 128), R("se", 0, 128))
        for t in range(3):
            ts(R("bt", 256 * t, 256 * t + 256, 4), PS(0, 0, 64), 0.0, A.is_gt, D(32 + t), A.mult)
        qz(R("qb"), R("sb"), R("bt"))
        mm(1, 192, R("q1"), R("s1"), R("qb"), R("sb"))
        scan(R("kc"), R("mk"), PS(1, 0, 192), 0.0, A.add, A.max)
        ts(R(so, 0, 12), R("kc", 15, 192, 16), D(17), A.subtract)
        send(R(lo, 0, 12), R(so, 0, 12), "ar%d" % r, dst, ne)
        for b in range(4):
            mm(4 + b, 128, R("qw", 128 * b, 128 * b + 128), R("sw", 128 * b, 128 * b + 128), R("qe", 0, 128), R("se", 0, 128))
            act(R("ht", b, 256, 4), PS(4 + b, 0, 64), AF.Copy, 0.03125)
        qz(R(qh), R(sh), R("ht"))
        send(CAST(R("lq", z, z + 64), dt.uint8), CAST(R(qh, 0, 64), dt.uint8), "ah%d" % r, dst, 2 * ne)
        send(R("ls", z, z + 64), R(sh, 0, 64), "ah%d" % r, dst, 2 * ne)
        for t in range(1, 4):
            gather_e(t, 0, 256, 1)
        gather_e(0, 0, 128, 0)
        gather_e(0, 128, 256, 0)
        for t in range(4):
            gather_e(t, 256, 448, t > 1)
        for k, (c0, c1) in enumerate(HALF):
            q, s = pack_e(c0, c1)
            ba, bb = ((2, 3), (0, 1))[k]
            mm(ba, c1 - c0, R("qua"), R("sua"), q, s)
            mm(bb, c1 - c0, R("qub"), R("sub"), q, s)
            if k == 0:
                act(R("ab", 2 * c0 + 1, 2 * c1, 2), PS(ba, 0, c1 - c0), AF.Sign, D(54), D(55))
            else:
                ts(R("ab", 2 * c0 + 1, 2 * c1, 2), PS(ba, 0, c1 - c0), 0.0, A.is_gt, cA, A.is_equal)
            act(R("ab", 2 * c0, 2 * c1, 2), PS(bb, 0, c1 - c0), AF.Sign, D(36), D(37))
            scan(R("oh", 2 * c0, 2 * c1), R("d01", 0, 2 * (c1 - c0)), R("ab", 2 * c0, 2 * c1), 0.0, A.max, A.min)
            act(R("at", 4 * c0 + 1, 4 * c1, 4), R("oh", 2 * c0 + 1, 2 * c1, 2), AF.Relu)
        for k, (c0, c1) in enumerate(HALF):
            off = R("om", c0 // 16, c1 // 16)
            tt(R("at", 4 * c0, 4 * c1, 4), IND(R("oh"), off), R("at", 4 * c0 + 1, 4 * c1, 4), A.max)
            act(R("at", 4 * c0 + 2, 4 * c1, 4), IND(R("oh"), off), AF.Relu)
        for k, (c0, c1) in enumerate(((0, 256), (256, 480))):
            qz(R("qa", c0, c1), R("sa", c0, c1), R("at", 4 * c0, 4 * c1))
            for ch in (2 * k, 2 * k + 1):
                c = (0, 128, 256, 352)[ch]
                mm(ch, 176, R("qa", c, c + 128), R("sa", c, c + 128), R("qc"), R("sc"))
        old, new = V(r % 2), V(1 - r % 2)
        L = [R(lo, 4 * t, 4 * t + 4) for t in range(3)]
        W = lambda ch, t: R("tb", 176 * ch + 64 * t, 176 * ch + 64 * t + (64 if t < 2 else 16))
        for ch in range(4):
            act(R("tb", 176 * ch, 176 * ch + 176), PS(ch, 0, 176))
            act(R("g0", 64 * ch, 64 * ch + 64), IND(W(ch, 0), L[0]))
        act(R("sm", 96, 192), IND(R("tb"), Lsm))
        for t in range(3):
            tt(R("hh", 80 * t, 80 * t + 64), IND(R("iot", 0, 64), L[t]), R("hk"), A.add)
            tt(R("dd", 80 * t + 1, 80 * t + 65), R("hh", 80 * t, 80 * t + 64), R("hh", 80 * t + 1, 80 * t + 65), A.subtract)
        for ch in range(4):
            tt(R("g1", 64 * ch, 64 * ch + 64), IND(W(ch, 1), L[1]), R("g0", 64 * ch, 64 * ch + 64), A.add)
            tt(R("tt", 80 * ch, 80 * ch + 64), IND(W(ch, 2), L[2]), R("g1", 64 * ch, 64 * ch + 64), A.add)
            for t in range(3):
                c = 65 * (3 * ch + t)
                scan(R("ro", c, c + 65), R("dd", 80 * t, 80 * t + 65), R("tt", 80 * ch, 80 * ch + 65), BIG, A.add, A.max)
        cp(R("ri", 0, 12), R("ro", 64, 780, 65))
        ts(R("ni", 0, 12), R("ri", 0, 12), 6, A.logical_shift_right, 63, A.bitwise_and)
        for k in range(3):
            ts(R("fi", k, 36, 3), R("ri", 0, 12), 2 * k, A.logical_shift_right, 3, A.bitwise_and)
        tt(V48(5), IND(R("ni", 0, 12), Ln), R("jb", 64 * r, 64 * r + 48), A.add)
        f = R("fi", 0, 36)
        tt(V(8), f, V(2), A.is_equal)
        tt(V(6), f, V(2), A.not_equal)
        tt(V(10), V(8), old, A.mult)
        tt(V(7), f, V(3), A.not_equal)
        tt(V(9), V(6), V(5), A.mult)
        act(R("c1p"), IND(V(10), Lent))
        tt(V(11), V(9), V(7), A.mult)
        tt(R("pre"), IND(V(11), Lent), R("c1p"), A.add)
        tr(R("v0"), R("pre"))
        tr(R("vb"), R("pre"))
        if r < 2:
            tt(new, V(11), V(10), A.add)
        else:
            act(R("fo"), R("v0"), AF.Sign)
            for k in range(7):
                dma("y", T.ofl[:, 64 * k:64 * k + 64], R("fo", 0, 64, 1, 16 * k, 16 * k + 8))
        for b in range(4):
            mm(4 + b, 128, R("qd", 128 * b, 128 * b + 128), R("sd", 128 * b, 128 * b + 128), R("lq", z, z + 128), R("ls", z, z + 128))
            c = 640 * b + 448 + 64 * r
            act(R("pl", c, c + 64), PS(4 + b, 0, 64))
        inherit(r == 2)

    for half, (c0, c1) in enumerate(((0, 320), (320, 448))):
        for t in range(4):
            gather_e(t, c0, c1, t if half == 0 else t > 0)
        q, s = pack_e(c0, c1)
        mm(half, c1 - c0, R("qv"), R("sv"), q, s)
        dma("y", T.oc[:, 4 * c0:4 * c1], CAST(q, dt.uint8))
        cp(R("yo", c0, c1), PS(half, 0, c1 - c0))
        dma("y" if half else "s", T.y[:, c0:c1], R("yo", c0, c1))
    for k in range(4):
        dma("s" if k % 2 else "y", T.osc[4 * k:4 * k + 4, :], R("se", 128, 576, 1, 32 * k, 32 * k + 4))
    issue()
    for s, v in count.items():
        wait("g", (s, v))
